import numpy as np, ml_dtypes
CORES = [16,17,18,19,32,33,34,35]
N = 8
BF = ml_dtypes.bfloat16
def f(rng, *shape):
    return (rng.standard_normal(shape, dtype=np.float32) * np.exp2(rng.integers(-2, 3, shape[:-1] + (1,)))).astype(BF)
def wide(rng, *shape):
    v = f(rng, *shape).astype(np.float32); k = shape[:-2] + (1, shape[-1])
    return (v * np.exp2(rng.integers(-6, 7, k)) * (rng.random(k) > 0.0625)).astype(BF)
def gentries(a):
    return np.ascontiguousarray(a.reshape(8, 16, -1).transpose(0, 2, 1)).reshape(8, -1)
def gtable(e):
    e = np.asarray(e); return np.ascontiguousarray(e.reshape(8, -1, 16).transpose(0, 2, 1)).reshape(128, -1).astype(np.int32)
E, S, D, F, R, V = 1024, 256, 64, 4, 4, 16384
W = E + (N - 1) * S
def arrive(a, snd):
    out = []
    for r in range(N):
        part = [a[r]]
        for t in range(1, N):
            q = (r + t) % N; p = gentries(snd[q]).reshape(8, N - 1, S)[:, N - 1 - t]
            part.append(np.take_along_axis(a[q], p[:, None, :], axis=2))
        out.append(np.concatenate(part, axis=2))
    return np.stack(out)
def slots(rng, lo, hi):
    return np.stack([rng.permuted(np.tile(np.arange(lo, hi), (8 * (N - 1), 1)), axis=1)[:, :S].reshape(8, N - 1, S) for r in range(N)])
def preds(rng):
    v = np.where(rng.random((N, 8, F, E)) < 0.5, rng.integers(0, E, (N, 8, F, E)), rng.integers(E, W, (N, 8, F, E)))
    v[:, :, 1] = np.where(rng.random((N, 8, E)) < 0.0625, v[:, :, 0], v[:, :, 1]); return v
def nodes(rng):
    return rng.integers(0, V, (N, 8, E))
def codes(rng):
    return rng.integers(0, D, (N, 8, E))
def make(rng, v, p, s, c):
    snd = np.stack([gtable(p[r].reshape(8, -1)) for r in range(N)]); a = arrive(s[:, :, None, :], snd)
    sf = np.take_along_axis(a, v.reshape(N, 8, 1, F * E), axis=3).reshape(N, 8, F, E)
    d = np.take_along_axis(sf, rng.integers(0, F, (N, 8, 1, E)), axis=2)[:, :, 0]; u = rng.integers(0, 8, (N, 8, E))
    d = np.where(u < 5, d, np.where(u < 7, d ^ 1, rng.integers(0, V, (N, 8, E))))
    return {"x": f(rng, N, 128, E), "tab": (rng.random((N, 128, D * D), dtype=np.float32) * 2 - 1).astype(BF), "dirs": c.astype(np.int32), "srcs": s.astype(np.int32), "dsts": d.astype(np.int32),
            "nb": np.stack([gtable(v[r].reshape(8, -1)) for r in range(N)]), "snd": snd}
def setup_inputs(rng):
    return make(rng, preds(rng), slots(rng, 0, E), nodes(rng), codes(rng))
def setup_inputs_ends(rng):
    p = slots(rng, 1, E - 1); p[..., 0] = E - 1; p[..., S - 1] = 0
    v = np.where(rng.random((N, 8, F, E)) < 0.75, rng.choice(np.array([0, 1, E - 1, E, E + S - 1, E + S, W - S, W - 1]), (N, 8, F, E)), preds(rng))
    return make(rng, v, p, rng.choice(np.array([0, 1, V - 2, V - 1]), (N, 8, E)), rng.choice(np.array([0, 1, D - 2, D - 1]), (N, 8, E)))
def setup_inputs_back(rng):
    s = 2 * rng.integers(0, V // 2, (1, 8, 1)) + rng.integers(0, 2, (N, 8, E))
    return make(rng, preds(rng), slots(rng, 0, E), s, codes(rng))
def setup_inputs_far(rng):
    v = rng.integers(E, W, (N, 8, F, E)); a = rng.permutation(N); t = int(rng.integers(0, N - 1))
    v[a[0]] = E + t * S + rng.integers(0, S, (8, F, E)); v[a[1]] = rng.integers(0, E, (8, F, E))
    p = slots(rng, 0, E); p[:] = p[:, :, :1].copy()
    return make(rng, v, p, nodes(rng), codes(rng))
def setup_inputs_alike(rng):
    v = preds(rng); v[:] = v[:, :, :1].copy()
    c = np.broadcast_to(rng.integers(0, D, (N, 8, 1)), (N, 8, E))
    return make(rng, v, slots(rng, 0, E), nodes(rng), c)
def setup_inputs_spread(rng):
    d = setup_inputs(rng); d["x"] = wide(rng, N, 128, E); return d
def check_inputs(d):
    bad = []
    for name, top in (("nb", W), ("snd", E), ("dirs", D), ("srcs", V), ("dsts", V)):
        if not ((d[name] >= 0) & (d[name] < top)).all(): bad.append(name + " in its range")
    p = np.stack([gentries(d["snd"][r]).reshape(8 * (N - 1), S) for r in range(N)])
    if not (np.diff(np.sort(p, axis=2), axis=2) > 0).all(): bad.append("different edges in the slots of a pair and group")
    if not (np.abs(d["x"].astype(np.float64)) <= 2.0 ** 40).all(): bad.append("x finite and at most 2**40 in size")
    if not (np.abs(d["tab"].astype(np.float64)) <= 1).all(): bad.append("tab at most 1 in size")
    return bad
def reference(x, tab, dirs, srcs, dsts, nb, snd):
    xs = x.astype(np.float64).reshape(N, 8, 16, E); v = np.stack([gentries(nb[r]) for r in range(N)])
    df = np.take_along_axis(arrive(dirs[:, :, None, :], snd)[:, :, 0], v, axis=2)
    sf = np.take_along_axis(arrive(srcs[:, :, None, :], snd)[:, :, 0], v, axis=2)
    off = D * df + np.tile(dirs, (1, 1, F)); back = sf == np.tile(dsts, (1, 1, F))
    w = []
    for r in range(N):
        c = np.take_along_axis(tab[r].astype(np.float64).reshape(8, 16, D * D), off[r][:, None, :], axis=2)
        w.append(np.where(back[r][:, None, :], 0.0, c * 0.25))
    m = xs
    for k in range(R):
        a = arrive(m, snd); new = []
        for r in range(N):
            term = w[r] * np.take_along_axis(a[r], v[r][:, None, :], axis=2)
            new.append(np.maximum(xs[r] + np.sum(term.reshape(8, 16, F, E), axis=2), 0.0))
        m = np.stack(new)
    return {"y": m.reshape(N, 128, E).astype(np.float32)}

@@ -1,0 +1,520 @@
+from concourse.bass import DstId, RemoteDMATransfer
+from concourse.mybir import AluOpType, ActivationFunctionType
+
+E, S, D, F, V, NR, SIM = 1024, 256, 64, 4, 16384, 8, 64
+W = E + (NR - 1) * S
+NS = (NR - 1) * S
+H = E // 2
+SQ = S // 4
+
+WAYS_X = ("BBAA", ("CCCB", "CCCB"))
+WAYS_M = ("BAAA", ("CCCB", "CCBB"))
+WAYS = [None, WAYS_X, WAYS_M, WAYS_M, WAYS_M]
+PE_FIRST = (3, 2)
+PE_LATER = (2, 2)
+
+SCRATCH = {
+    "CI": ("sbuf", [128, 512], "int32"), "CB": ("sbuf", [128, 512], "bfloat16"),
+    "RL": ("sbuf", [128, 512], "bfloat16"), "ZX": ("sbuf", [128, 144], "bfloat16"),
+    "ZY": ("sbuf", [128, 144], "bfloat16"), "ZI": ("sbuf", [128, 160], "bfloat16"),
+    "IF": ("sbuf", [128, 128], "float32"),
+    "sndi": ("sbuf", [128, 112], "int32"), "sndu": ("sbuf", [128, 112], "uint16"),
+    "nbi": ("sbuf", [128, 256], "int32"), "nbu": ("sbuf", [128, 256], "uint16"),
+    "offu": ("sbuf", [128, 256], "uint16"), "zt": ("sbuf", [128, 256], "float32"),
+    "ot": ("sbuf", [128, 256], "float32"), "bL": ("sbuf", [128, 128], "float32"),
+    "dL": ("sbuf", [128, 128], "float32"),
+    "DW": ("sbuf", [128, E], "bfloat16"),
+    "C0": ("sbuf", [128, (NR - 1) * SQ], "bfloat16"), "L0": ("sbuf", [128, (NR - 1) * SQ], "bfloat16"),
+    "W0": ("sbuf", [128, W], "bfloat16"), "W1": ("sbuf", [128, W], "bfloat16"),
+    "W2": ("sbuf", [128, W], "float32"), "W3": ("sbuf", [128, W], "float32"), "W4": ("sbuf", [128, W], "float32"),
+    "B0": ("sbuf", [128, NS], "bfloat16"), "B1": ("sbuf", [128, NS], "bfloat16"),
+    "B2": ("sbuf", [128, NS], "float32"), "B3": ("sbuf", [128, NS], "float32"), "B4": ("sbuf", [128, NS], "float32"),
+    "GM": ("sbuf", [128, F * E], "bfloat16"), "XG": ("sbuf", [128, F * E], "bfloat16"),
+    "wt": ("sbuf", [128, F * E], "bfloat16"), "tabw": ("sbuf", [128, D * D + 16], "bfloat16"),
+    "P": ("sbuf", [128, F * E], "float32"), "GB": ("sbuf", [128, F * E], "float32"),
+    "SM": ("sbuf", [128, E], "float32"), "YB": ("sbuf", [128, E], "float32"),
+}
+for _b in range(8):
+    SCRATCH["pb%d" % _b] = ("psum", [128, 512], "float32")
+
+SEMAPHORES = (["cv", "ca", "ct", "cg", "sent", "mfar", "mnear"] + ["arr%d" % k for k in range(1, 5)]
+              + ["d%d" % k for k in range(14)] + ["rl%d_%d" % (k, j) for k in range(1, 5) for j in range(4)])
+
+
+def bits(engs):
+    m = 0
+    for e in engs:
+        m |= 1 << e
+    return m
+
+
+def split(sets, n):
+    while len(sets) < n:
+        big = max(range(len(sets)), key=lambda q: (len(sets[q]), q))
+        s0 = sets.pop(big)
+        sets += [s0[:len(s0) // 2], s0[len(s0) // 2:]]
+    return sets
+
+
+def sides(T, topo, c):
+    cores = list(T.cores)
+    near = [d for d in cores if topo.chip(d) == topo.chip(c)]
+    far = [d for d in cores if topo.chip(d) != topo.chip(c)]
+    i = near.index(c)
+    lo = topo.engines(c, far[0])
+    hi = [e for e in topo.engines(c, near[(i + 1) % len(near)]) if e not in lo]
+    return near, far, i, lo, hi
+
+
+def small_plan(T, topo, c):
+    near, far, i, lo, hi = sides(T, topo, c)
+    fa = [far[(i + j) % len(far)] for j in range(len(far))]
+    ne = [near[(i + j) % len(near)] for j in range(1, len(near))]
+    return list(zip(fa, split([lo], len(fa)))), list(zip(ne, split([hi], len(ne))))
+
+
+def make_plan(T, topo, k):
+    cores = list(T.cores)
+    n = len(cores)
+    calls, relay, arr = {}, {}, {c: 0 for c in cores}
+    for r, c in enumerate(cores):
+        near, far, i, lo, hi = sides(T, topo, c)
+        over = [z for z in topo.cores_of(c) if topo.die(z) != topo.die(c) and z not in cores]
+
+        def mate_side(a):
+            return [z for z in range(SIM) if z not in cores and topo.chip(z) != topo.chip(a)
+                    and topo.mates(topo.chip(z), topo.chip(far[0])) and topo.die(z) == topo.die(a)
+                    and topo.may_write(a, z) and topo.may_write(z, far[0])]
+        owners = [a for a in near if mate_side(a)]
+        ways = WAYS[k][1][owners.index(c) % len(WAYS[k][1])] if c in owners else WAYS[k][0]
+        off, on, nb = [], [], 0
+        for j, way in enumerate(ways):
+            d = far[(i + j) % len(far)]
+            if way == "A":
+                off.append((d, None))
+            elif way == "C":
+                zs = mate_side(c)
+                off.append((d, zs[owners.index(c) % len(zs)]))
+            else:
+                on.append((d, over[(i + 2 * nb) % len(over)]))
+                nb += 1
+        for j in range(1, len(near)):
+            on.append((near[(i + j) % len(near)], None))
+        ncall = max(len(off), (len(off) + len(on)) // 2)
+        pad = [None] * (ncall - len(off))
+        off = pad + off if ways[0] == "B" else off + pad
+        mine = []
+        for j in range(ncall):
+            tr = []
+            sets = [hi]
+            if off[j] is not None:
+                tr.append((off[j], lo))
+            else:
+                sets = [lo, hi]
+            if j == ncall - 1:
+                sets = split(sets, len(on))
+            for s0 in sets:
+                if on:
+                    tr.append((on.pop(0), s0))
+            out = []
+            for (d, z), engs in tr:
+                t = (cores.index(d) - r) % n
+                col = E + (n - t - 1) * S
+                if z is None:
+                    arr[d] += len(engs)
+                    out.append({"t": t, "to": d, "engs": engs, "col": col, "z": None})
+                else:
+                    ent = {"t": t, "to": z, "engs": engs, "col": col, "z": z, "dst": d, "key": (j, r)}
+                    relay.setdefault(z, []).append(ent)
+                    arr[d] += len(topo.engines(z, d))
+                    out.append(ent)
+            mine.append(out)
+        calls[c] = mine
+    for z in relay:
+        relay[z].sort(key=lambda e: e["key"])
+        for j, e in enumerate(relay[z]):
+            e["slot"] = j
+    return calls, relay, arr
+
+
+def helper_program(g, core, T, topo, plans):
+    sent = 0
+    for k in range(1, 5):
+        for e in plans[k][1].get(core, []):
+            j = e["slot"]
+            g.wait_ge(T.sem["rl%d_%d" % (k, j)], len(e["engs"]))
+            rid, pid, _ = topo.addr(e["dst"])
+            g.remote_dma(T["W%d" % k][:, e["col"]:e["col"] + S], T["B%d" % k][:, j * S:(j + 1) * S],
+                         T.sem["arr%d" % k], T.sem.sent, pid, rid, topo.mask(core, e["dst"]))
+            sent += len(topo.engines(core, e["dst"]))
+    if sent:
+        g.wait_ge(T.sem.sent, sent)
+
+
+def rank_program(g, core, T, topo):
+    plans = [None] + [make_plan(T, topo, k) for k in range(1, 5)]
+    rank = T.rank_of(core)
+    if rank is None:
+        helper_program(g, core, T, topo, plans)
+        return
+    A, ACT = AluOpType, ActivationFunctionType
+    Q = {"g": g, "v": g.vector, "a": g.scalar, "t": g.tensor, "s": g.sync}
+    known = {q: {} for q in Q}
+    total, snap, hist = {}, {}, {}
+    ndma = [0]
+
+    def order(q, reads, writes):
+        need = {}
+        for lst, wr in ((reads, False), (writes, True)):
+            for key, lo, hi in lst:
+                ps = key.startswith("pb")
+                for (l2, h2, w2, q2, tok) in hist.get(key, []):
+                    if ps:
+                        hit = (q2 != q) or (q != "t" and (wr or w2) and l2 < hi and lo < h2)
+                    else:
+                        hit = (wr or w2) and l2 < hi and lo < h2
+                    if hit:
+                        need[tok[0]] = max(need.get(tok[0], 0), tok[1])
+        for sem, val in sorted(need.items(), key=lambda kv: -len(snap.get(kv, {}))):
+            if known[q].get(sem, 0) < val:
+                Q[q].wait_ge(T.sem[sem], val)
+                known[q][sem] = val
+                for s2, v2 in snap.get((sem, val), {}).items():
+                    if known[q].get(s2, 0) < v2:
+                        known[q][s2] = v2
+
+    def note(q, reads, writes, tok):
+        snap[tok] = dict(known[q])
+        for key, lo, hi in writes:
+            keep = [h for h in hist.get(key, []) if not (lo <= h[0] and h[1] <= hi)]
+            hist[key] = keep + [(lo, hi, True, q, tok)]
+        for key, lo, hi in reads:
+            hist.setdefault(key, []).append((lo, hi, False, q, tok))
+
+    def op(q, fn, reads, writes):
+        order(q, reads, writes)
+        sem = "c" + q
+        total[sem] = total.get(sem, 0) + 1
+        fn().then_inc(T.sem[sem], 1)
+        note(q, reads, writes, (sem, total[sem]))
+
+    def dma(q, out, in_, reads, writes):
+        order(q, reads, writes)
+        sem = "d%d" % ndma[0]
+        ndma[0] += 1
+        total[sem] = 16
+        Q[q].dma_start(out, in_).then_inc(T.sem[sem], 16)
+        note(q + "d", reads, writes, (sem, 16))
+
+    known["sd"], known["ad"] = known["s"], known["a"]
+    vec, act, pe = g.vector, g.scalar, g.tensor
+    pb = [T["pb%d" % b] for b in range(8)]
+    IB, IBK = T.ZI[:, 16:144], ("ZI", 0, 160)
+
+    def mm(b, lo, hi, lhsT, rhs, start, stop, reads):
+        op("t", lambda: pe.matmul(pb[b][:, lo:hi], lhsT, rhs, start, stop), reads, [("pb%d" % b, lo, hi)])
+
+    def evict(q, name, a, b, lo, n):
+        if q == "a":
+            fn = lambda: act.activation(T[name][:, a:a + n], pb[b][:, lo:lo + n], ACT.Copy)
+        else:
+            fn = lambda: vec.tensor_copy(T[name][:, a:a + n], pb[b][:, lo:lo + n])
+        op(q, fn, [("pb%d" % b, lo, lo + n)], [(name, a, a + n)])
+
+    def gather(q, out, okey, win, wkey, offs, fkey, scale=None, relu=False):
+        src = win.indirect(offs)
+        if q == "a":
+            if relu:
+                fn = lambda: act.activation(out, src, ACT.Relu)
+            elif scale is None:
+                fn = lambda: act.activation(out, src, ACT.Copy)
+            else:
+                fn = lambda: act.activation(out, src, ACT.Copy, scale=scale)
+        elif relu:
+            fn = lambda: vec.tensor_scalar(out, src, 0.0, None, A.max)
+        elif scale is None:
+            fn = lambda: vec.tensor_copy(out, src)
+        else:
+            fn = lambda: vec.tensor_scalar(out, src, scale, None, A.mult)
+        op(q, fn, [wkey, fkey], [okey])
+
+    def piece(q, k, wname, t, relu):
+        a = (t - 1) * S
+        gather(q, T["B%d" % k][:, a:a + S], ("B%d" % k, a, a + S), T[wname][:, 0:E], (wname, 0, E),
+               T.sndu[:, a // 16:(a + S) // 16], ("sndu", 0, 112), relu=relu)
+
+    def send(trs):
+        order("g", [x[4] for x in trs], [])
+        out = []
+        for to, engs, sem, src, _, dst in trs:
+            rid, pid, _ = topo.addr(to)
+            out.append(RemoteDMATransfer(dst_ids=[DstId(rid=rid, pnc=pid)], dma_engine_mask=bits(engs),
+                                         remote_sem=T.sem[sem], src=src, dst=dst))
+            total["sent"] = total.get("sent", 0) + len(engs)
+        g.remote_dma_fused(out, local_sem=T.sem.sent)
+
+    def exchange(k, wname, relu, lo=0, hi=9, who="va"):
+        B = T["B%d" % k]
+        n = 0
+        for call in plans[k][0][core][lo:hi]:
+            for e in call:
+                piece(who[n % len(who)], k, wname, e["t"], relu)
+                n += 1
+        for call in plans[k][0][core][lo:hi]:
+            trs = []
+            for e in call:
+                a = (e["t"] - 1) * S
+                if e["z"] is None:
+                    dst, sem = T["W%d" % k][:, e["col"]:e["col"] + S], "arr%d" % k
+                else:
+                    dst, sem = B[:, e["slot"] * S:(e["slot"] + 1) * S], "rl%d_%d" % (k, e["slot"])
+                trs.append((e["to"], e["engs"], sem, B[:, a:a + S], ("B%d" % k, a, a + S), dst))
+            send(trs)
+        if lo == 0:
+            total["arr%d" % k] = plans[k][2][core]
+            hist.setdefault("W%d" % k, []).append((E, W, True, "r", ("arr%d" % k, plans[k][2][core])))
+
+    dma("s", T.CI[32:64, 0:256], T.srcs[:], [], [("CI1", 0, 256)])
+    dma("a", T.sndi[:], T.snd[:], [], [("sndi", 0, 112)])
+    dma("s", T.CI[64:96, 0:256], T.srcs[:], [], [("CI2", 0, 256)])
+    dma("a", T.CI[0:32, 0:256], T.dirs[:], [], [("CI0", 0, 256)])
+    dma("a", T.W1[:, 0:E], T.x[:], [], [("W1", 0, E)])
+    dma("s", T.nbi[:], T.nb[:], [], [("nbi", 0, 256)])
+    dma("s", T.CI[32:64, 256:512], T.dsts[:], [], [("CI1", 256, 512)])
+    dma("s", T.CI[64:96, 256:512], T.dsts[:], [], [("CI2", 256, 512)])
+    dma("s", T.tabw[:, 0:D * D], T.tab[:], [], [("tabw", 0, D * D)])
+
+    for name, n, val in (("RL", 512, 1.0), ("ZI", 160, 1.0), ("ZX", 144, float(D)), ("ZY", 144, 1.0)):
+        op("v", lambda name=name, val=val: vec.memset(T[name][:], val), [], [(name, 0, n)])
+    op("v", lambda: vec.memset(T.CI[0:32, 256:512], 0), [], [("CI0", 256, 512)])
+    op("v", lambda: vec.memset(T.tabw[:, D * D:D * D + 16], 0.0), [], [("tabw", D * D, D * D + 16)])
+
+    def sel(name, n, pattern, cmp, base, cm):
+        op("g", lambda: g.affine_select(T[name][:], T[name][:], pattern, cmp, 0.0, base, cm), [(name, 0, n)], [(name, 0, n)])
+    sel("RL", 512, [[-1, 4], [-4, 8], [-32, 16]], A.is_equal, 0, 1)
+    sel("ZI", 160, [[-1, 160]], A.is_equal, 16, 1)
+    sel("ZX", 144, [[-16, 9], [1000, 16]], A.is_equal, -15000, 1)
+    sel("ZY", 144, [[-16, 9], [1000, 16]], A.is_ge, -15001, 1)
+    sel("ZY", 144, [[16, 9], [0, 16]], A.is_ge, 2, -1)
+
+    def rows(lo, b0, wname):
+        hi = lo + 256
+        op("v", lambda: vec.tensor_scalar(T.CI[32:64, lo:hi], T.CI[32:64, lo:hi], V - 128, None, A.bitwise_and),
+           [("CI1", lo, hi)], [("CI1", lo, hi)])
+        op("v", lambda: vec.tensor_scalar(T.CI[64:96, lo:hi], T.CI[64:96, lo:hi], 127, None, A.bitwise_and),
+           [("CI2", lo, hi)], [("CI2", lo, hi)])
+        op("v", lambda: vec.tensor_copy(T.CB[0:96, lo:hi], T.CI[0:96, lo:hi]),
+           [("CI0", lo, hi), ("CI1", lo, hi), ("CI2", lo, hi)], [("CB", lo, hi)])
+        for q in range(4):
+            mm(b0 + q // 2, (q % 2) * 256, (q % 2) * 256 + 256, T.RL[0:96, q * 128:(q + 1) * 128], T.CB[0:96, lo:hi],
+               True, True, [("RL", 0, 512), ("CB", lo, hi)])
+        evict("a", wname, 0, b0, 0, H)
+        evict("v", wname, H, b0 + 1, 0, H)
+
+    op("v", lambda: vec.tensor_copy(T.sndu[:], T.sndi[:]), [("sndi", 0, 112)], [("sndu", 0, 112)])
+    exchange(1, "W1", False, 0, 1, "a")
+    rows(0, 0, "W0")
+
+    cores = list(T.cores)
+    mine = small_plan(T, topo, core)
+    for part, sem, bank0 in ((mine[0], "mfar", 2), (mine[1], "mnear", 4)):
+        ts = [(cores.index(d) - rank) % NR for d, _ in part]
+        c0 = 0 if sem == "mfar" else len(mine[0]) * SQ
+        half = (len(ts) + 1) // 2
+        turn = sorted(range(len(ts)), key=lambda j: (j % half, j))
+        for j in turn:
+            piece("va"[j // half], 0, "W0", ts[j], False)
+        for j in turn:
+            for q in range(4):
+                a = (ts[j] - 1) * S + q * SQ
+                mm(bank0 + j // half, (j % half) * SQ, (j % half + 1) * SQ, T.ZI[:, 16 - 4 * q:144 - 4 * q],
+                   T.B0[:, a:a + SQ], q == 0, q == 3, [IBK, ("B0", a, a + SQ)])
+        evict("v", "C0", c0, bank0, 0, half * SQ)
+        evict("a", "C0", c0 + half * SQ, bank0 + 1, 0, (len(ts) - half) * SQ)
+        send([(d, engs, sem, T.C0[:, c0 + j * SQ:c0 + (j + 1) * SQ], ("C0", c0 + j * SQ, c0 + (j + 1) * SQ),
+               T.L0[:, (NR - ts[j] - 1) * SQ:(NR - ts[j]) * SQ]) for j, (d, engs) in enumerate(part)])
+    landed = {"mfar": [], "mnear": []}
+    for q0 in cores:
+        for part, sem in zip(small_plan(T, topo, q0), ("mfar", "mnear")):
+            for d, engs in part:
+                if d == core:
+                    total[sem] = total.get(sem, 0) + len(engs)
+                    landed[sem].append((cores.index(q0) - rank) % NR - 1)
+    for sem in landed:
+        for tt in landed[sem]:
+            hist.setdefault("L0", []).append((tt * SQ, tt * SQ + SQ, True, "r", (sem, total[sem])))
+    exchange(1, "W1", False, 1, 9, "av")
+
+    rows(256, 6, "DW")
+    op("v", lambda: vec.tensor_copy(T.IF[:], IB), [IBK], [("IF", 0, 128)])
+    op("v", lambda: vec.tensor_copy(T.nbu[:], T.nbi[:]), [("nbi", 0, 256)], [("nbu", 0, 256)])
+    for b, zn, wn in ((0, "ZX", "W0"), (1, "ZY", "DW")):
+        for h in range(16):
+            mm(b, 0, 64, T[zn][:, 15 - h:143 - h], T[wn][:, h:E:16], h == 0, h == 15, [(zn, 0, 144), (wn, 0, E)])
+    for u in range(2):
+        for c in range(2):
+            a = (u * 2 + c) * 32
+            op("a", lambda a=a, u=u: act.activation(T.bL[:, a:a + 32], pb[0][:, u * 32:u * 32 + 32], ACT.Copy, scale=1.0 / D),
+               [("pb0", 0, 64)], [("bL", a, a + 32)])
+            op("v", lambda a=a, u=u: vec.tensor_scalar(T.dL[:, a:a + 32], pb[1][:, u * 32:u * 32 + 32], -1.0, None, A.mult),
+               [("pb1", 0, 64)], [("dL", a, a + 32)])
+
+    nb0 = 0
+    for sem in ("mnear", "mfar"):
+        for j, tt in enumerate(landed[sem]):
+            bank = 2 + (nb0 + j) % 6
+            for q in range(4):
+                mm(bank, q * SQ, (q + 1) * SQ, T.ZI[:, 16 + 4 * q:144 + 4 * q], T.L0[:, tt * SQ:(tt + 1) * SQ], True, True,
+                   [IBK, ("L0", tt * SQ, (tt + 1) * SQ)])
+            evict("av"[j % 2], "W0", E + tt * S, bank, 0, S)
+        nb0 = 3
+
+    def term(u, c):
+        a, b = (u * F + c) * H, c * 64 + u * 32
+        return a, a + H, T.nbu[:, b:b + 32], ("nbu", 0, 256)
+
+    xb, yb = (6, 2), (7, 3)
+    for u in range(2):
+        for c in range(F):
+            a, b, offs, fk = term(u, c)
+            gather("av"[c % 2], T.GM[:, a:b], ("GM", a, b), T.W0[:], ("W0", 0, W), offs, fk)
+    for u in range(2):
+        for s2 in range(2):
+            k0 = u * 128 + s2 * 64
+            for bank, zn, own in ((yb[u], "ZY", "dL"), (xb[u], "ZX", "bL")):
+                mm(bank, s2 * 64, s2 * 64 + 64, T.IF[:], T[own][:, u * 64:u * 64 + 64], True, False,
+                   [("IF", 0, 128), (own, u * 64, u * 64 + 64)])
+                for h in range(16):
+                    mm(bank, s2 * 64, s2 * 64 + 64, T[zn][:, 15 - h:143 - h], T.GM[:, 16 * k0 + h:16 * (k0 + 64):16],
+                       False, h == 15, [(zn, 0, 144), ("GM", 16 * k0, 16 * k0 + 1024)])
+
+    def offsets(u):
+        a, b = u * 128, u * 128 + 128
+        op("v", lambda: vec.tensor_scalar(T.zt[:, a:b], pb[yb[u]][:, 0:128], 0.0, float(D * D), A.is_equal, A.mult),
+           [("pb%d" % yb[u], 0, 128)], [("zt", a, b)])
+        op("v", lambda: vec.tensor_tensor(T.ot[:, a:b], pb[xb[u]][:, 0:128], T.zt[:, a:b], A.max),
+           [("pb%d" % xb[u], 0, 128), ("zt", a, b)], [("ot", a, b)])
+        op("v", lambda: vec.tensor_copy(T.offu[:, a:b], T.ot[:, a:b]), [("ot", a, b)], [("offu", a, b)])
+
+    def pe_x(u):
+        mm(u, 0, H, IB, T.W1[:, u * H:u * H + H], True, False, [IBK, ("W1", u * H, u * H + H)])
+
+    def pe_add(u, c, stop):
+        a = (u * F + c) * H
+        mm(u, 0, H, T.IF[:], T.P[:, a:a + H], False, stop, [("IF", 0, 128), ("P", a, a + H)])
+
+    def v_add(u, c, last, parts=1):
+        a = (u * F + c) * H
+        n = H // parts
+        for p in range(parts):
+            lo = p * n
+            if last:
+                op("v", lambda lo=lo: vec.tensor_tensor(T.SM[:, u * H + lo:u * H + lo + n], pb[u][:, lo:lo + n],
+                                                        T.P[:, a + lo:a + lo + n], A.add),
+                   [("pb%d" % u, lo, lo + n), ("P", a + lo, a + lo + n)], [("SM", u * H + lo, u * H + lo + n)])
+            else:
+                op("v", lambda lo=lo: vec.tensor_tensor(pb[u][:, lo:lo + n], pb[u][:, lo:lo + n],
+                                                        T.P[:, a + lo:a + lo + n], A.add),
+                   [("P", a + lo, a + lo + n)], [("pb%d" % u, lo, lo + n)])
+
+    def keep_own(k):
+        wn = "W%d" % k
+        op("a", lambda: act.activation(T[wn][:, 0:H], T.SM[:, 0:H], ACT.Relu), [("SM", 0, H)], [(wn, 0, H)])
+        op("v", lambda: vec.tensor_scalar(T[wn][:, H:E], T.SM[:, H:E], 0.0, None, A.max), [("SM", H, E)], [(wn, H, E)])
+
+    for u in range(2):
+        for c in range(F):
+            a, b, offs, fk = term(u, c)
+            gather("a", T.XG[:, a:b], ("XG", a, b), T.W1[:], ("W1", 0, W), offs, fk, scale=0.25)
+
+    def first(u, c):
+        a = (u * F + c) * H
+        op("v", lambda: vec.tensor_tensor(T.P[:, a:a + H], T.tabw[:].indirect(T.offu[:, a // 16:(a + H) // 16]),
+                                          T.XG[:, a:a + H], A.mult),
+           [("tabw", 0, D * D + 16), ("offu", a // 16, (a + H) // 16), ("XG", a, a + H)], [("P", a, a + H)])
+        if c < PE_FIRST[u]:
+            pe_add(u, c, c == PE_FIRST[u] - 1)
+    pe_x(0)
+    pe_x(1)
+    offsets(0)
+    for c in range(F):
+        first(0, c)
+    offsets(1)
+    first(1, 0)
+    first(1, 1)
+    for c in range(PE_FIRST[0], F):
+        v_add(0, c, c == F - 1)
+    first(1, 2)
+    if PE_FIRST[1] <= 2:
+        v_add(1, 2, False)
+    first(1, 3)
+    v_add(1, 3, True)
+    exchange(2, "SM", True)
+    keep_own(2)
+
+    for u in range(2):
+        for c in range(F):
+            a = (u * F + c) * H
+            gather("av"[c % 2], T.wt[:, a:a + H], ("wt", a, a + H), T.tabw[:], ("tabw", 0, D * D + 16),
+                   T.offu[:, a // 16:(a + H) // 16], ("offu", a // 16, (a + H) // 16), scale=0.25)
+            if c < 3:
+                mm(2 + u * 3 + c, 0, H, IB, T.wt[:, a:a + H], True, True, [IBK, ("wt", a, a + H)])
+
+    for k in range(2, 5):
+        wn = "W%d" % k
+        final = k == 4
+        pe_x(0)
+        pe_x(1)
+        for u, c in ((0, 0), (0, 1), (0, 2), (1, 0), (1, 1), (1, 2)):
+            a, b, offs, fk = term(u, c)
+            gather("a", T.GB[:, a:b], ("GB", a, b), T[wn][:], (wn, 0, W), offs, fk)
+
+        def fused(u):
+            a, b, offs, fk = term(u, 3)
+            op("v", lambda: vec.tensor_tensor(T.P[:, a:b], T[wn][:].indirect(offs), T.wt[:, a:b], A.mult),
+               [(wn, 0, W), fk, ("wt", a, b)], [("P", a, b)])
+
+        def mul(u, c):
+            a, bank = (u * F + c) * H, 2 + u * 3 + c
+            op("v", lambda: vec.tensor_tensor(T.P[:, a:a + H], pb[bank][:], T.GB[:, a:a + H], A.mult),
+               [("pb%d" % bank, 0, H), ("GB", a, a + H)], [("P", a, a + H)])
+        n0, n1 = PE_LATER
+        fused(0)
+        pe_add(0, 3, n0 == 1)
+        mul(0, 0)
+        if n0 >= 2:
+            pe_add(0, 0, n0 == 2)
+        fused(1)
+        mul(0, 1)
+        if n0 >= 3:
+            pe_add(0, 1, True)
+        pe_add(1, 3, n1 == 1)
+        mul(0, 2)
+        mul(1, 0)
+        if n1 >= 2:
+            pe_add(1, 0, n1 == 2)
+        for c in range(n0 - 1, 3):
+            v_add(0, c, c == 2)
+        if final:
+            op("a", lambda: act.activation(T.YB[:, 0:H], T.SM[:, 0:H], ACT.Relu), [("SM", 0, H)], [("YB", 0, H)])
+            dma("s", T.y[:, 0:H], T.YB[:, 0:H], [("YB", 0, H)], [])
+        mul(1, 1)
+        if n1 >= 3:
+            pe_add(1, 1, True)
+        for c in range(n1 - 1, 2):
+            v_add(1, c, False)
+        mul(1, 2)
+        if not final:
+            v_add(1, 2, True)
+            exchange(k + 1, "SM", True)
+            keep_own(k + 1)
+        else:
+            v_add(1, 2, True, parts=2)
+            m = H + H // 2
+            op("a", lambda: act.activation(T.YB[:, H:m], T.SM[:, H:m], ACT.Relu), [("SM", H, m)], [("YB", H, m)])
+            op("v", lambda: vec.tensor_scalar(T.YB[:, m:E], T.SM[:, m:E], 0.0, None, A.max), [("SM", m, E)], [("YB", m, E)])
+            dma("a", T.y[:, H:m], T.YB[:, H:m], [("YB", H, m)], [])
+            dma("s", T.y[:, m:E], T.YB[:, m:E], [("YB", m, E)], [])
+
+    for sem in sorted(total):
+        g.wait_ge(T.sem[sem], total[sem])

@@ -6,39 +6,62 @@ W = E + (NR - 1) * S
 NS = (NR - 1) * S
 H = E // 2
 SQ = S // 4
+SH = S // 2
+HP = 64
+TW = D * D + 16
+STREAMS = "ab"
+CH = ((0, 384), (384, 704), (704, 896), (896, 1024))
+LATER = [str(k) + s for k in range(2, 5) for s in STREAMS]
+NODE = 2.0 ** -9
+ROUND64 = 1.5 * 2.0 ** 29
+GM_A = 576
 
-WAYS_X = ("BBAA", ("CCCB", "CCCB"))
-WAYS_M = ("BAAA", ("CCCB", "CCBB"))
-WAYS = [None, WAYS_X, WAYS_M, WAYS_M, WAYS_M]
-PE_FIRST = (3, 2)
-PE_LATER = (2, 2)
+PLAN_X = (("B|B", "A|n", "A|nn"), (("C|B", "C|n", "A|nn"), ("C|B", "C|n", "A|nn")))
+PLAN_M = (("A|B", "A|n", "A|nn"), (("C|B", "C|B", "n|nn"), ("C|B", "C|B", "n|nn")))
+X_EARLY = 2
+LATE = 3
+WHO_M = "avaaaaa"
+EARLY = (0, 0, 0, 0)
+NCOPY = 2
+NB = 1
 
 SCRATCH = {
     "CI": ("sbuf", [128, 512], "int32"), "CB": ("sbuf", [128, 512], "bfloat16"),
-    "RL": ("sbuf", [128, 512], "bfloat16"), "ZX": ("sbuf", [128, 144], "bfloat16"),
-    "ZY": ("sbuf", [128, 144], "bfloat16"), "ZI": ("sbuf", [128, 160], "bfloat16"),
-    "IF": ("sbuf", [128, 128], "float32"),
-    "sndi": ("sbuf", [128, 112], "int32"), "sndu": ("sbuf", [128, 112], "uint16"),
+    "RL": ("sbuf", [128, 512], "bfloat16"), "ZZ": ("sbuf", [128, 144], "bfloat16"),
+    "ZI": ("sbuf", [128, 160], "bfloat16"), "I4": ("sbuf", [128, 128], "bfloat16"),
+    "IF": ("sbuf", [128, 128], "float32"), "DD": ("sbuf", [128, 128], "bfloat16"),
+    "SF": ("sbuf", [128, 128], "float32"), "SW": ("sbuf", [128, 128], "float32"),
+    "SB": ("sbuf", [128, 128], "bfloat16"),
+    "sndi": ("sbuf", [128, NR - 1, 16], "int32"), "sndu": ("sbuf", [128, 112], "uint16"),
     "nbi": ("sbuf", [128, 256], "int32"), "nbu": ("sbuf", [128, 256], "uint16"),
-    "offu": ("sbuf", [128, 256], "uint16"), "zt": ("sbuf", [128, 256], "float32"),
-    "ot": ("sbuf", [128, 256], "float32"), "bL": ("sbuf", [128, 128], "float32"),
-    "dL": ("sbuf", [128, 128], "float32"),
+    "f1": ("sbuf", [128, 128], "int32"), "f2": ("sbuf", [128, 128], "int32"), "f3": ("sbuf", [128, 128], "int32"),
+    "rt": ("sbuf", [128, 256], "bfloat16"), "et": ("sbuf", [128, 256], "bfloat16"),
+    "ro": ("sbuf", [128, 64], "float32"), "bL": ("sbuf", [128, 128], "bfloat16"), "dL": ("sbuf", [128, 64], "float32"),
     "DW": ("sbuf", [128, E], "bfloat16"),
     "C0": ("sbuf", [128, (NR - 1) * SQ], "bfloat16"), "L0": ("sbuf", [128, (NR - 1) * SQ], "bfloat16"),
-    "W0": ("sbuf", [128, W], "bfloat16"), "W1": ("sbuf", [128, W], "bfloat16"),
-    "W2": ("sbuf", [128, W], "float32"), "W3": ("sbuf", [128, W], "float32"), "W4": ("sbuf", [128, W], "float32"),
-    "B0": ("sbuf", [128, NS], "bfloat16"), "B1": ("sbuf", [128, NS], "bfloat16"),
-    "B2": ("sbuf", [128, NS], "float32"), "B3": ("sbuf", [128, NS], "float32"), "B4": ("sbuf", [128, NS], "float32"),
-    "GM": ("sbuf", [128, F * E], "bfloat16"), "XG": ("sbuf", [128, F * E], "bfloat16"),
-    "wt": ("sbuf", [128, F * E], "bfloat16"), "tabw": ("sbuf", [128, D * D + 16], "bfloat16"),
-    "P": ("sbuf", [128, F * E], "float32"), "GB": ("sbuf", [128, F * E], "float32"),
-    "SM": ("sbuf", [128, E], "float32"), "YB": ("sbuf", [128, E], "float32"),
+    "W0": ("sbuf", [128, W], "bfloat16"), "Wx": ("sbuf", [128, 2 * W], "bfloat16"),
+    "B0": ("sbuf", [128, NS], "bfloat16"), "Bx": ("sbuf", [128, NS], "bfloat16"),
+    "GM": ("sbuf", [128, F * E], "bfloat16"),
 }
+for _s in STREAMS:
+    SCRATCH["snd" + _s] = ("sbuf", [128, 56], "uint16")
+    for _n in ("nx", "nm", "of"):
+        SCRATCH[_n + _s] = ("sbuf", [128, 128], "uint16")
+    SCRATCH["tb" + _s] = ("sbuf", [128, TW], "bfloat16")
+    SCRATCH["D0" + _s] = ("sbuf", [128, 2 * E], "bfloat16")
+    SCRATCH["w1" + _s] = ("sbuf", [128, E], "bfloat16")
+    SCRATCH["D1" + _s] = ("sbuf", [128, 2 * E], "float32")
+    SCRATCH["Q" + _s] = ("sbuf", [128, 2 * E], "float32")
+    SCRATCH["Y" + _s] = ("sbuf", [128, E], "float32")
+for _x in LATER:
+    SCRATCH["W" + _x] = ("sbuf", [128, W], "float32")
+    SCRATCH["B" + _x] = ("sbuf", [128, NS // 2], "float32")
 for _b in range(8):
     SCRATCH["pb%d" % _b] = ("psum", [128, 512], "float32")
 
-SEMAPHORES = (["cv", "ca", "ct", "cg", "sent", "mfar", "mnear"] + ["arr%d" % k for k in range(1, 5)]
-              + ["d%d" % k for k in range(14)] + ["rl%d_%d" % (k, j) for k in range(1, 5) for j in range(4)])
+SEMAPHORES = (["cv", "ca", "ct", "cg", "sent", "sentx", "mfar", "mnear"] + ["d%d" % k for k in range(30)]
+              + ["ar%s_%d" % (x, t) for x in ["x"] + LATER for t in range(NR - 1)]
+              + ["rl%s_%d" % (x, j) for x in ["x"] + LATER for j in range(4)])
 
 
 def bits(engs):
@@ -73,86 +96,84 @@ def small_plan(T, topo, c):
     return list(zip(fa, split([lo], len(fa)))), list(zip(ne, split([hi], len(ne))))
 
 
-def make_plan(T, topo, k):
+def make_plan(T, topo, plan):
     cores = list(T.cores)
     n = len(cores)
-    calls, relay, arr = {}, {}, {c: 0 for c in cores}
+    calls, relay, arr = {}, {}, {c: [] for c in cores}
     for r, c in enumerate(cores):
         near, far, i, lo, hi = sides(T, topo, c)
         over = [z for z in topo.cores_of(c) if topo.die(z) != topo.die(c) and z not in cores]
-
-        def mate_side(a):
-            return [z for z in range(SIM) if z not in cores and topo.chip(z) != topo.chip(a)
-                    and topo.mates(topo.chip(z), topo.chip(far[0])) and topo.die(z) == topo.die(a)
-                    and topo.may_write(a, z) and topo.may_write(z, far[0])]
-        owners = [a for a in near if mate_side(a)]
-        ways = WAYS[k][1][owners.index(c) % len(WAYS[k][1])] if c in owners else WAYS[k][0]
-        off, on, nb = [], [], 0
-        for j, way in enumerate(ways):
-            d = far[(i + j) % len(far)]
-            if way == "A":
-                off.append((d, None))
-            elif way == "C":
-                zs = mate_side(c)
-                off.append((d, zs[owners.index(c) % len(zs)]))
-            else:
-                on.append((d, over[(i + 2 * nb) % len(over)]))
-                nb += 1
-        for j in range(1, len(near)):
-            on.append((near[(i + j) % len(near)], None))
-        ncall = max(len(off), (len(off) + len(on)) // 2)
-        pad = [None] * (ncall - len(off))
-        off = pad + off if ways[0] == "B" else off + pad
-        mine = []
-        for j in range(ncall):
-            tr = []
-            sets = [hi]
-            if off[j] is not None:
-                tr.append((off[j], lo))
-            else:
-                sets = [lo, hi]
-            if j == ncall - 1:
-                sets = split(sets, len(on))
-            for s0 in sets:
-                if on:
-                    tr.append((on.pop(0), s0))
+        beyond = [z for z in range(SIM) if z not in cores and topo.mates(topo.chip(z), topo.chip(far[0]))
+                  and topo.may_write(z, far[0])]
+        beyond.sort(key=lambda z: topo.die(z) != topo.die(c))
+        owners = [a for a in near if topo.may_write(a, beyond[0])]
+        mine = plan[1][owners.index(c) % len(plan[1])] if c in owners else plan[0]
+        used = {"far": 0, "n": 0, "B": 0, "C": 0}
+        calls[c] = []
+        for j, call in enumerate(mine):
             out = []
-            for (d, z), engs in tr:
-                t = (cores.index(d) - r) % n
-                col = E + (n - t - 1) * S
-                if z is None:
-                    arr[d] += len(engs)
-                    out.append({"t": t, "to": d, "engs": engs, "col": col, "z": None})
-                else:
-                    ent = {"t": t, "to": z, "engs": engs, "col": col, "z": z, "dst": d, "key": (j, r)}
-                    relay.setdefault(z, []).append(ent)
-                    arr[d] += len(topo.engines(z, d))
+            for ways, engines in zip(call.split("|"), (lo, hi)):
+                for way, engs in zip(ways, split([engines], len(ways))):
+                    z = None
+                    if way == "n":
+                        used["n"] += 1
+                        d = near[(i + used["n"]) % len(near)]
+                    else:
+                        d = far[(i + used["far"]) % len(far)]
+                        used["far"] += 1
+                    if way == "B":
+                        z = over[(i + 2 * used["B"]) % len(over)]
+                        used["B"] += 1
+                    elif way == "C":
+                        z = beyond[(owners.index(c) + len(owners) * used["C"]) % len(beyond)]
+                        used["C"] += 1
+                    t = (cores.index(d) - r) % n
+                    ent = {"t": t, "to": d, "engs": engs, "tt": n - t - 1, "z": z}
+                    if z is None:
+                        arr[d].append((j + (0.5 if way == "A" else 0), n - t - 1, len(engs)))
+                    else:
+                        ent.update({"to": z, "dst": d, "key": (j, r)})
+                        relay.setdefault(z, []).append(ent)
+                        arr[d].append((j + LATE, n - t - 1, len(topo.engines(z, d))))
                     out.append(ent)
-            mine.append(out)
-        calls[c] = mine
+            calls[c].append(out)
     for z in relay:
         relay[z].sort(key=lambda e: e["key"])
         for j, e in enumerate(relay[z]):
             e["slot"] = j
+    for c in cores:
+        arr[c].sort()
     return calls, relay, arr
+
+
+def landing(T, x, tt):
+    col = E + tt * S
+    if x == "x":
+        return T.Wx[:, col:col + S], "arx_%d" % tt
+    return T["W" + x][:, col:col + SH], "ar%s_%d" % (x, tt)
 
 
 def helper_program(g, core, T, topo, plans):
     sent = 0
-    for k in range(1, 5):
-        for e in plans[k][1].get(core, []):
+    for x in ["x"] + LATER:
+        n = S if x == "x" else SH
+        for e in plans[x][1].get(core, []):
             j = e["slot"]
-            g.wait_ge(T.sem["rl%d_%d" % (k, j)], len(e["engs"]))
+            g.wait_ge(T.sem["rl%s_%d" % (x, j)], len(e["engs"]))
             rid, pid, _ = topo.addr(e["dst"])
-            g.remote_dma(T["W%d" % k][:, e["col"]:e["col"] + S], T["B%d" % k][:, j * S:(j + 1) * S],
-                         T.sem["arr%d" % k], T.sem.sent, pid, rid, topo.mask(core, e["dst"]))
+            dst, sem = landing(T, x, e["tt"])
+            g.remote_dma(dst, T["B" + x][:, j * n:(j + 1) * n], T.sem[sem], T.sem.sent, pid, rid,
+                         topo.mask(core, e["dst"]))
             sent += len(topo.engines(core, e["dst"]))
     if sent:
         g.wait_ge(T.sem.sent, sent)
 
 
 def rank_program(g, core, T, topo):
-    plans = [None] + [make_plan(T, topo, k) for k in range(1, 5)]
+    plans = {"x": make_plan(T, topo, PLAN_X)}
+    plan_m = make_plan(T, topo, PLAN_M)
+    for x in LATER:
+        plans[x] = plan_m
     rank = T.rank_of(core)
     if rank is None:
         helper_program(g, core, T, topo, plans)
@@ -210,129 +231,154 @@ def rank_program(g, core, T, topo):
     vec, act, pe = g.vector, g.scalar, g.tensor
     pb = [T["pb%d" % b] for b in range(8)]
     IB, IBK = T.ZI[:, 16:144], ("ZI", 0, 160)
+    half = (slice(0, HP), slice(HP, 2 * HP))
+    NCH = range(len(CH))
 
     def mm(b, lo, hi, lhsT, rhs, start, stop, reads):
         op("t", lambda: pe.matmul(pb[b][:, lo:hi], lhsT, rhs, start, stop), reads, [("pb%d" % b, lo, hi)])
 
-    def evict(q, name, a, b, lo, n):
+    def evict(q, name, a, b, lo, n, relu=False):
+        out, src = T[name][:, a:a + n], pb[b][:, lo:lo + n]
         if q == "a":
-            fn = lambda: act.activation(T[name][:, a:a + n], pb[b][:, lo:lo + n], ACT.Copy)
+            fn = lambda: act.activation(out, src, ACT.Relu if relu else ACT.Copy)
+        elif relu:
+            fn = lambda: vec.tensor_scalar(out, src, 0.0, None, A.max)
         else:
-            fn = lambda: vec.tensor_copy(T[name][:, a:a + n], pb[b][:, lo:lo + n])
+            fn = lambda: vec.tensor_copy(out, src)
         op(q, fn, [("pb%d" % b, lo, lo + n)], [(name, a, a + n)])
 
-    def gather(q, out, okey, win, wkey, offs, fkey, scale=None, relu=False):
+    def gather(q, out, okey, win, wkeys, offs, fkeys, scale=None):
         src = win.indirect(offs)
         if q == "a":
-            if relu:
-                fn = lambda: act.activation(out, src, ACT.Relu)
-            elif scale is None:
+            if scale is None:
                 fn = lambda: act.activation(out, src, ACT.Copy)
             else:
                 fn = lambda: act.activation(out, src, ACT.Copy, scale=scale)
-        elif relu:
-            fn = lambda: vec.tensor_scalar(out, src, 0.0, None, A.max)
         elif scale is None:
             fn = lambda: vec.tensor_copy(out, src)
         else:
             fn = lambda: vec.tensor_scalar(out, src, scale, None, A.mult)
-        op(q, fn, [wkey, fkey], [okey])
+        op(q, fn, wkeys + fkeys, [okey])
 
-    def piece(q, k, wname, t, relu):
-        a = (t - 1) * S
-        gather(q, T["B%d" % k][:, a:a + S], ("B%d" % k, a, a + S), T[wname][:, 0:E], (wname, 0, E),
-               T.sndu[:, a // 16:(a + S) // 16], ("sndu", 0, 112), relu=relu)
+    def piece(q, x, t):
+        if x in ("0", "x"):
+            a, n, offs, fk = (t - 1) * S, S, T.sndu[:, (t - 1) * 16:t * 16], [("sndu", 0, 112)]
+        else:
+            a, n, offs = (t - 1) * SH, SH, T["snd" + x[1]][:, (t - 1) * 8:t * 8]
+            fk = [("snd%s%d" % (x[1], h), 0, 56) for h in range(2)]
+        gather(q, T["B" + x][:, a:a + n], ("B" + x, a, a + n), T["W" + x][:, 0:E], [("W" + x, 0, E)], offs, fk)
 
-    def send(trs):
+    def send(trs, local):
         order("g", [x[4] for x in trs], [])
         out = []
         for to, engs, sem, src, _, dst in trs:
             rid, pid, _ = topo.addr(to)
             out.append(RemoteDMATransfer(dst_ids=[DstId(rid=rid, pnc=pid)], dma_engine_mask=bits(engs),
                                          remote_sem=T.sem[sem], src=src, dst=dst))
-            total["sent"] = total.get("sent", 0) + len(engs)
-        g.remote_dma_fused(out, local_sem=T.sem.sent)
+            total[local] = total.get(local, 0) + len(engs)
+        g.remote_dma_fused(out, local_sem=T.sem[local])
 
-    def exchange(k, wname, relu, lo=0, hi=9, who="va"):
-        B = T["B%d" % k]
-        n = 0
-        for call in plans[k][0][core][lo:hi]:
-            for e in call:
-                piece(who[n % len(who)], k, wname, e["t"], relu)
-                n += 1
-        for call in plans[k][0][core][lo:hi]:
+    def pieces(x, who, lo=0, hi=NR):
+        for k, e in enumerate([e for call in plans[x][0][core] for e in call][lo:hi]):
+            piece(who[k % len(who)], x, e["t"])
+
+    def calls(x, lo=0, hi=NR):
+        B, n = T["B" + x], S if x == "x" else SH
+        for call in plans[x][0][core][lo:hi]:
             trs = []
             for e in call:
-                a = (e["t"] - 1) * S
+                a = (e["t"] - 1) * n
                 if e["z"] is None:
-                    dst, sem = T["W%d" % k][:, e["col"]:e["col"] + S], "arr%d" % k
+                    dst, sem = landing(T, x, e["tt"])
                 else:
-                    dst, sem = B[:, e["slot"] * S:(e["slot"] + 1) * S], "rl%d_%d" % (k, e["slot"])
-                trs.append((e["to"], e["engs"], sem, B[:, a:a + S], ("B%d" % k, a, a + S), dst))
-            send(trs)
-        if lo == 0:
-            total["arr%d" % k] = plans[k][2][core]
-            hist.setdefault("W%d" % k, []).append((E, W, True, "r", ("arr%d" % k, plans[k][2][core])))
+                    dst, sem = B[:, e["slot"] * n:(e["slot"] + 1) * n], "rl%s_%d" % (x, e["slot"])
+                trs.append((e["to"], e["engs"], sem, B[:, a:a + n], ("B" + x, a, a + n), dst))
+            send(trs, "sentx" if x == "x" else "sent")
+
+    def exchange(x, who):
+        pieces(x, who)
+        calls(x)
+        for _, tt, cnt in plans[x][2][core]:
+            sem = landing(T, x, tt)[1]
+            total[sem] = cnt
+            hist["W" + x].append((E + tt * S, E + tt * S + SH, True, "r", (sem, cnt)))
 
     dma("s", T.CI[32:64, 0:256], T.srcs[:], [], [("CI1", 0, 256)])
     dma("a", T.sndi[:], T.snd[:], [], [("sndi", 0, 112)])
-    dma("s", T.CI[64:96, 0:256], T.srcs[:], [], [("CI2", 0, 256)])
     dma("a", T.CI[0:32, 0:256], T.dirs[:], [], [("CI0", 0, 256)])
-    dma("a", T.W1[:, 0:E], T.x[:], [], [("W1", 0, E)])
-    dma("s", T.nbi[:], T.nb[:], [], [("nbi", 0, 256)])
+    dma("a", T.Wx[:, 0:E], T.x[:], [], [("Wx", 0, E)])
     dma("s", T.CI[32:64, 256:512], T.dsts[:], [], [("CI1", 256, 512)])
-    dma("s", T.CI[64:96, 256:512], T.dsts[:], [], [("CI2", 256, 512)])
-    dma("s", T.tabw[:, 0:D * D], T.tab[:], [], [("tabw", 0, D * D)])
+    dma("s", T.CI[0:32, 256:512], T.dirs[:], [], [("CI0", 256, 512)])
+    dma("s", T.nbi[:], T.nb[:], [], [("nbi", 0, 256)])
 
-    for name, n, val in (("RL", 512, 1.0), ("ZI", 160, 1.0), ("ZX", 144, float(D)), ("ZY", 144, 1.0)):
-        op("v", lambda name=name, val=val: vec.memset(T[name][:], val), [], [(name, 0, n)])
-    op("v", lambda: vec.memset(T.CI[0:32, 256:512], 0), [], [("CI0", 256, 512)])
-    op("v", lambda: vec.memset(T.tabw[:, D * D:D * D + 16], 0.0), [], [("tabw", D * D, D * D + 16)])
+    def load_tab(si, after):
+        for h in range(2):
+            dma("s", T["tb" + STREAMS[si]][half[h], 0:D * D], T.tab[half[si], :], after,
+                [("tb%s%d" % (STREAMS[si], h), 0, D * D)])
+    load_tab(0, [])
+    for h in range(2):
+        dma("s", T.Wx[half[h], W:W + E], T.x[half[1 - h], :], [], [("Vx%d" % h, 0, E)])
 
-    def sel(name, n, pattern, cmp, base, cm):
-        op("g", lambda: g.affine_select(T[name][:], T[name][:], pattern, cmp, 0.0, base, cm), [(name, 0, n)], [(name, 0, n)])
-    sel("RL", 512, [[-1, 4], [-4, 8], [-32, 16]], A.is_equal, 0, 1)
+    for name, n, val in (("ZI", 160, 1.0), ("RL", 512, 1.0), ("ZZ", 144, NODE)):
+        op("v", lambda: vec.memset(T[name][:], val), [], [(name, 0, n)])
+    for s in STREAMS:
+        op("v", lambda: vec.memset(T["tb" + s][:, D * D:TW], 0.0), [], [("tz" + s, 0, 16)])
+    for s in STREAMS:
+        op("v", lambda: vec.memset(T["D0" + s][:, 0:2 * E:2], 0.0), [], [("Dz" + s, 0, E)])
+
+    def sel(name, n, pattern, cmp, base, cm, fill=0.0):
+        op("g", lambda: g.affine_select(T[name][:], T[name][:], pattern, cmp, fill, base, cm), [(name, 0, n)], [(name, 0, n)])
     sel("ZI", 160, [[-1, 160]], A.is_equal, 16, 1)
-    sel("ZX", 144, [[-16, 9], [1000, 16]], A.is_equal, -15000, 1)
-    sel("ZY", 144, [[-16, 9], [1000, 16]], A.is_ge, -15001, 1)
-    sel("ZY", 144, [[16, 9], [0, 16]], A.is_ge, 2, -1)
+    sel("RL", 512, [[-1, 4], [-4, 8], [-32, 16]], A.is_equal, 0, 1)
+    sel("ZZ", 144, [[-16, 9], [1000, 16]], A.is_ge, -15000, 1)
+    sel("ZZ", 144, [[16, 9], [0, 16]], A.is_ge, 2, -1)
+    sel("ZZ", 144, [[-16, 9], [1000, 16]], A.not_equal, -15000, 1, float(D))
+    op("a", lambda: act.activation(T.IF[:], IB, ACT.Copy), [IBK], [("IF", 0, 128)])
+    op("a", lambda: act.activation(T.I4[:], IB, ACT.Copy, scale=float(D * D)), [IBK], [("I4", 0, 128)])
+    for h in range(2):
+        for m in range(2):
+            op("a", lambda: act.activation(T.DD[half[h], half[m]], T.ZI[half[h], 16 + h * HP:16 + (h + 1) * HP], ACT.Copy),
+               [IBK], [("DD%d" % h, m * HP, (m + 1) * HP)])
+    DDK = [("DD0", 0, 128), ("DD1", 0, 128)]
+    op("a", lambda: act.activation(T.SF[:], T.DD[:], ACT.Copy), DDK, [("SF", 0, 128)])
+    op("v", lambda: vec.tensor_tensor(T.SW[:], T.DD[:], IB, A.subtract), DDK + [IBK], [("SW", 0, 128)])
+    op("a", lambda: act.activation(T.SB[:], T.SW[:], ACT.Copy), [("SW", 0, 128)], [("SB", 0, 128)])
 
-    def rows(lo, b0, wname):
+    def rows(lo, b0, wname, who):
         hi = lo + 256
-        op("v", lambda: vec.tensor_scalar(T.CI[32:64, lo:hi], T.CI[32:64, lo:hi], V - 128, None, A.bitwise_and),
-           [("CI1", lo, hi)], [("CI1", lo, hi)])
-        op("v", lambda: vec.tensor_scalar(T.CI[64:96, lo:hi], T.CI[64:96, lo:hi], 127, None, A.bitwise_and),
-           [("CI2", lo, hi)], [("CI2", lo, hi)])
-        op("v", lambda: vec.tensor_copy(T.CB[0:96, lo:hi], T.CI[0:96, lo:hi]),
-           [("CI0", lo, hi), ("CI1", lo, hi), ("CI2", lo, hi)], [("CB", lo, hi)])
+        op("v", lambda: vec.tensor_copy(T.CB[0:64, lo:hi], T.CI[0:64, lo:hi]),
+           [("CI0", lo, hi), ("CI1", lo, hi)], [("CB0", lo, hi)])
+        op("v", lambda: vec.tensor_tensor(T.CB[64:96, lo:hi], T.CI[32:64, lo:hi], T.CB[32:64, lo:hi], A.subtract),
+           [("CI1", lo, hi), ("CB0", lo, hi)], [("CB1", lo, hi)])
         for q in range(4):
             mm(b0 + q // 2, (q % 2) * 256, (q % 2) * 256 + 256, T.RL[0:96, q * 128:(q + 1) * 128], T.CB[0:96, lo:hi],
-               True, True, [("RL", 0, 512), ("CB", lo, hi)])
-        evict("a", wname, 0, b0, 0, H)
-        evict("v", wname, H, b0 + 1, 0, H)
+               True, True, [("RL", 0, 512), ("CB0", lo, hi), ("CB1", lo, hi)])
+        evict(who[0], wname, 0, b0, 0, H)
+        evict(who[1], wname, H, b0 + 1, 0, H)
 
     op("v", lambda: vec.tensor_copy(T.sndu[:], T.sndi[:]), [("sndi", 0, 112)], [("sndu", 0, 112)])
-    exchange(1, "W1", False, 0, 1, "a")
-    rows(0, 0, "W0")
+    pieces("x", "a", 0, X_EARLY)
+    calls("x", 0, 1)
+    rows(0, 0, "W0", "va")
 
     cores = list(T.cores)
     mine = small_plan(T, topo, core)
     for part, sem, bank0 in ((mine[0], "mfar", 2), (mine[1], "mnear", 4)):
         ts = [(cores.index(d) - rank) % NR for d, _ in part]
         c0 = 0 if sem == "mfar" else len(mine[0]) * SQ
-        half = (len(ts) + 1) // 2
-        turn = sorted(range(len(ts)), key=lambda j: (j % half, j))
+        hf = (len(ts) + 1) // 2
+        turn = sorted(range(len(ts)), key=lambda j: (j % hf, j))
         for j in turn:
-            piece("va"[j // half], 0, "W0", ts[j], False)
+            piece("va"[j // hf], "0", ts[j])
         for j in turn:
             for q in range(4):
                 a = (ts[j] - 1) * S + q * SQ
-                mm(bank0 + j // half, (j % half) * SQ, (j % half + 1) * SQ, T.ZI[:, 16 - 4 * q:144 - 4 * q],
+                mm(bank0 + j // hf, (j % hf) * SQ, (j % hf + 1) * SQ, T.ZI[:, 16 - 4 * q:144 - 4 * q],
                    T.B0[:, a:a + SQ], q == 0, q == 3, [IBK, ("B0", a, a + SQ)])
-        evict("v", "C0", c0, bank0, 0, half * SQ)
-        evict("a", "C0", c0 + half * SQ, bank0 + 1, 0, (len(ts) - half) * SQ)
+        evict("v", "C0", c0, bank0, 0, hf * SQ)
+        evict("a", "C0", c0 + hf * SQ, bank0 + 1, 0, (len(ts) - hf) * SQ)
         send([(d, engs, sem, T.C0[:, c0 + j * SQ:c0 + (j + 1) * SQ], ("C0", c0 + j * SQ, c0 + (j + 1) * SQ),
-               T.L0[:, (NR - ts[j] - 1) * SQ:(NR - ts[j]) * SQ]) for j, (d, engs) in enumerate(part)])
+               T.L0[:, (NR - ts[j] - 1) * SQ:(NR - ts[j]) * SQ]) for j, (d, engs) in enumerate(part)], "sentx")
     landed = {"mfar": [], "mnear": []}
     for q0 in cores:
         for part, sem in zip(small_plan(T, topo, q0), ("mfar", "mnear")):
@@ -343,178 +389,253 @@ def rank_program(g, core, T, topo):
     for sem in landed:
         for tt in landed[sem]:
             hist.setdefault("L0", []).append((tt * SQ, tt * SQ + SQ, True, "r", (sem, total[sem])))
-    exchange(1, "W1", False, 1, 9, "av")
+    pieces("x", "av", X_EARLY)
+    calls("x", 1)
+    for _, tt, cnt in plans["x"][2][core]:
+        total["arx_%d" % tt] = cnt
+        hist["Wx"].append((E + tt * S, E + tt * S + S, True, "r", ("arx_%d" % tt, cnt)))
 
-    rows(256, 6, "DW")
-    op("v", lambda: vec.tensor_copy(T.IF[:], IB), [IBK], [("IF", 0, 128)])
+    rows(256, 6, "DW", "av")
     op("v", lambda: vec.tensor_copy(T.nbu[:], T.nbi[:]), [("nbi", 0, 256)], [("nbu", 0, 256)])
-    for b, zn, wn in ((0, "ZX", "W0"), (1, "ZY", "DW")):
-        for h in range(16):
-            mm(b, 0, 64, T[zn][:, 15 - h:143 - h], T[wn][:, h:E:16], h == 0, h == 15, [(zn, 0, 144), (wn, 0, E)])
+    load_tab(1, [("nbu", 0, 256)])
+    late = [tt for when, tt, _ in plans["x"][2][core] if when >= LATE]
+    runs = []
+    for tt in range(NR - 1):
+        if tt in late:
+            continue
+        if runs and runs[-1][1] == tt:
+            runs[-1][1] += 1
+        else:
+            runs.append([tt, tt + 1])
+    for lo, hi in runs:
+        a, b = E + lo * S, E + hi * S
+        for h in range(2):
+            dma("s", T.Wx[half[h], W + a:W + b], T.Wx[half[1 - h], a:b], [("Wx", a, b)], [("Vx%d" % h, a, b)])
+    for si, s in enumerate(STREAMS):
+        for h in range(2):
+            op("v", lambda: vec.tensor_scalar(T["nx" + s][half[h], :], T.nbi[half[si], h * 128:(h + 1) * 128],
+                                              float(0 if h == si else W), None, A.add),
+               [("nbi", 0, 256)], [("nx%s%d" % (s, h), 0, 128)])
+    for h in range(16):
+        mm(0, 0, 64, T.ZZ[:, 15 - h:143 - h], T.DW[:, h:E:16], h == 0, h == 15, [("ZZ", 0, 144), ("DW", 0, E)])
+    op("v", lambda: vec.tensor_scalar(T.ro[:], pb[0][:, 0:64], ROUND64, ROUND64, A.add, A.subtract),
+       [("pb0", 0, 64)], [("ro", 0, 64)])
+    op("v", lambda: vec.tensor_tensor(T.dL[:], T.ro[:], pb[0][:, 0:64], A.subtract), [("pb0", 0, 64), ("ro", 0, 64)],
+       [("dL", 0, 64)])
     for u in range(2):
-        for c in range(2):
-            a = (u * 2 + c) * 32
-            op("a", lambda a=a, u=u: act.activation(T.bL[:, a:a + 32], pb[0][:, u * 32:u * 32 + 32], ACT.Copy, scale=1.0 / D),
-               [("pb0", 0, 64)], [("bL", a, a + 32)])
-            op("v", lambda a=a, u=u: vec.tensor_scalar(T.dL[:, a:a + 32], pb[1][:, u * 32:u * 32 + 32], -1.0, None, A.mult),
-               [("pb1", 0, 64)], [("dL", a, a + 32)])
+        op("a", lambda: act.activation(T.bL[:, u * 64:u * 64 + 64], T.ro[:], ACT.Copy, scale=1.0 / D), [("ro", 0, 64)],
+           [("bL", u * 64, u * 64 + 64)])
 
     nb0 = 0
     for sem in ("mnear", "mfar"):
         for j, tt in enumerate(landed[sem]):
-            bank = 2 + (nb0 + j) % 6
+            bank = 1 + nb0 + j
             for q in range(4):
                 mm(bank, q * SQ, (q + 1) * SQ, T.ZI[:, 16 + 4 * q:144 + 4 * q], T.L0[:, tt * SQ:(tt + 1) * SQ], True, True,
                    [IBK, ("L0", tt * SQ, (tt + 1) * SQ)])
             evict("av"[j % 2], "W0", E + tt * S, bank, 0, S)
         nb0 = 3
 
-    def term(u, c):
-        a, b = (u * F + c) * H, c * 64 + u * 32
-        return a, a + H, T.nbu[:, b:b + 32], ("nbu", 0, 256)
+    def meta(c):
+        for q, a, b in (("a", c * E, c * E + GM_A), ("v", c * E + GM_A, (c + 1) * E)):
+            gather(q, T.GM[:, a:b], ("GM", a, b), T.W0[:], [("W0", 0, W)], T.nbu[:, a // 16:b // 16], [("nbu", 0, 256)])
 
-    xb, yb = (6, 2), (7, 3)
-    for u in range(2):
-        for c in range(F):
-            a, b, offs, fk = term(u, c)
-            gather("av"[c % 2], T.GM[:, a:b], ("GM", a, b), T.W0[:], ("W0", 0, W), offs, fk)
-    for u in range(2):
-        for s2 in range(2):
-            k0 = u * 128 + s2 * 64
-            for bank, zn, own in ((yb[u], "ZY", "dL"), (xb[u], "ZX", "bL")):
-                mm(bank, s2 * 64, s2 * 64 + 64, T.IF[:], T[own][:, u * 64:u * 64 + 64], True, False,
-                   [("IF", 0, 128), (own, u * 64, u * 64 + 64)])
-                for h in range(16):
-                    mm(bank, s2 * 64, s2 * 64 + 64, T[zn][:, 15 - h:143 - h], T.GM[:, 16 * k0 + h:16 * (k0 + 64):16],
-                       False, h == 15, [(zn, 0, 144), ("GM", 16 * k0, 16 * k0 + 1024)])
+    def turn_meta(c):
+        lo = (c // 2) * 64
+        mm(4 + c % 2, lo, lo + 64, T.IF[:], T.dL[:], True, False, [("IF", 0, 128), ("dL", 0, 64)])
+        for h in range(16):
+            mm(4 + c % 2, lo, lo + 64, T.ZZ[:, 15 - h:143 - h], T.GM[:, c * E + h:(c + 1) * E:16],
+               False, h == 15, [("ZZ", 0, 144), ("GM", c * E, (c + 1) * E)])
 
-    def offsets(u):
-        a, b = u * 128, u * 128 + 128
-        op("v", lambda: vec.tensor_scalar(T.zt[:, a:b], pb[yb[u]][:, 0:128], 0.0, float(D * D), A.is_equal, A.mult),
-           [("pb%d" % yb[u], 0, 128)], [("zt", a, b)])
-        op("v", lambda: vec.tensor_tensor(T.ot[:, a:b], pb[xb[u]][:, 0:128], T.zt[:, a:b], A.max),
-           [("pb%d" % xb[u], 0, 128), ("zt", a, b)], [("ot", a, b)])
-        op("v", lambda: vec.tensor_copy(T.offu[:, a:b], T.ot[:, a:b]), [("ot", a, b)], [("offu", a, b)])
+    def offsets(j):
+        a, b = j * 128, j * 128 + 128
+        z, zk = pb[4 + j][:, 0:128], ("pb%d" % (4 + j), 0, 128)
+        op("v", lambda: vec.tensor_scalar(T.rt[:, a:b], z, ROUND64, ROUND64, A.add, A.subtract), [zk], [("rt", a, b)])
+        op("v", lambda: vec.tensor_tensor(T.et[:, a:b], z, T.rt[:, a:b], A.is_equal), [zk, ("rt", a, b)], [("et", a, b)])
+        mm(6 + j, 0, 128, IB, T.bL[:], True, False, [IBK, ("bL", 0, 128)])
+        mm(6 + j, 0, 128, IB, T.rt[:, a:b], False, False, [IBK, ("rt", a, b)])
+        mm(6 + j, 0, 128, T.I4[:], T.et[:, a:b], False, True, [("I4", 0, 128), ("et", a, b)])
 
-    def pe_x(u):
-        mm(u, 0, H, IB, T.W1[:, u * H:u * H + H], True, False, [IBK, ("W1", u * H, u * H + H)])
+    def offset_lists(j, si):
+        s = STREAMS[si]
+        for h in range(2):
+            op("v", lambda: vec.tensor_scalar(T["of" + s][half[h], j * 64:j * 64 + 64], pb[6 + j][half[si], h * 64:h * 64 + 64],
+                                              float(D * D), None, A.min),
+               [("pb%d" % (6 + j), h * 64, h * 64 + 64)], [("of%s%d" % (s, h), j * 64, j * 64 + 64)])
 
-    def pe_add(u, c, stop):
-        a = (u * F + c) * H
-        mm(u, 0, H, T.IF[:], T.P[:, a:a + H], False, stop, [("IF", 0, 128), ("P", a, a + H)])
+    def later_lists():
+        v, vk = T.nbi[:, 128:256], ("nbi", 0, 256)
+        op("v", lambda: vec.tensor_scalar(T.f1[:], v, SH, None, A.bitwise_and), [vk], [("f1", 0, 128)])
+        op("v", lambda: vec.tensor_scalar(T.f2[:], v, float(E), None, A.is_ge), [vk], [("f2", 0, 128)])
+        op("v", lambda: vec.tensor_scalar(T.f1[:], T.f1[:], -2.0, float(SH), A.mult, A.add), [("f1", 0, 128)], [("f1", 0, 128)])
+        for si, s in enumerate(STREAMS):
+            op("v", lambda: vec.tensor_copy(T["nm" + s][half[0], :], T.nbi[half[si], 0:128]), [vk], [("nm%s0" % s, 0, 128)])
+        op("v", lambda: vec.tensor_tensor(T.f3[:], T.f1[:], T.f2[:], A.mult), [("f1", 0, 128), ("f2", 0, 128)], [("f3", 0, 128)])
+        op("v", lambda: vec.tensor_tensor(T.f2[:], T.f3[:], v, A.add), [("f3", 0, 128), vk], [("f2", 0, 128)])
+        for si, s in enumerate(STREAMS):
+            op("v", lambda: vec.tensor_copy(T["nm" + s][half[1], :], T.f2[half[si], :]), [("f2", 0, 128)], [("nm%s1" % s, 0, 128)])
 
-    def v_add(u, c, last, parts=1):
-        a = (u * F + c) * H
-        n = H // parts
-        for p in range(parts):
-            lo = p * n
-            if last:
-                op("v", lambda lo=lo: vec.tensor_tensor(T.SM[:, u * H + lo:u * H + lo + n], pb[u][:, lo:lo + n],
-                                                        T.P[:, a + lo:a + lo + n], A.add),
-                   [("pb%d" % u, lo, lo + n), ("P", a + lo, a + lo + n)], [("SM", u * H + lo, u * H + lo + n)])
-            else:
-                op("v", lambda lo=lo: vec.tensor_tensor(pb[u][:, lo:lo + n], pb[u][:, lo:lo + n],
-                                                        T.P[:, a + lo:a + lo + n], A.add),
-                   [("P", a + lo, a + lo + n)], [("pb%d" % u, lo, lo + n)])
+    def listed(name, s, j, i):
+        a, b = CH[i]
+        lo, hi = j * 64 + a // 16, j * 64 + b // 16
+        return T[name + s][:, lo:hi], [("%s%s%d" % (name, s, h), lo, hi) for h in range(2)]
 
-    def keep_own(k):
-        wn = "W%d" % k
-        op("a", lambda: act.activation(T[wn][:, 0:H], T.SM[:, 0:H], ACT.Relu), [("SM", 0, H)], [(wn, 0, H)])
-        op("v", lambda: vec.tensor_scalar(T[wn][:, H:E], T.SM[:, H:E], 0.0, None, A.max), [("SM", H, E)], [(wn, H, E)])
+    def wplace(s, j, i):
+        a, b = CH[i]
+        if j == 0:
+            return T["D0" + s][:, 2 * a + 1:2 * b:2], ("Dw" + s, a, b)
+        return T["w1" + s][:, a:b], ("w1" + s, a, b)
 
-    for u in range(2):
-        for c in range(F):
-            a, b, offs, fk = term(u, c)
-            gather("a", T.XG[:, a:b], ("XG", a, b), T.W1[:], ("W1", 0, W), offs, fk, scale=0.25)
+    def term(s, j, i):
+        a, b = CH[i]
+        return T["D1" + s][:, 2 * a + j:2 * b:2], ("D1%s%d" % (s, j), a, b)
 
-    def first(u, c):
-        a = (u * F + c) * H
-        op("v", lambda: vec.tensor_tensor(T.P[:, a:a + H], T.tabw[:].indirect(T.offu[:, a // 16:(a + H) // 16]),
-                                          T.XG[:, a:a + H], A.mult),
-           [("tabw", 0, D * D + 16), ("offu", a // 16, (a + H) // 16), ("XG", a, a + H)], [("P", a, a + H)])
-        if c < PE_FIRST[u]:
-            pe_add(u, c, c == PE_FIRST[u] - 1)
-    pe_x(0)
-    pe_x(1)
-    offsets(0)
-    for c in range(F):
-        first(0, c)
+    def window(k, s):
+        if k == 1:
+            return T.Wx[:], [("Wx", 0, 2 * W), ("Vx0", 0, W), ("Vx1", 0, W)], "nx"
+        return T["W%d%s" % (k, s)][:], [("W%d%s" % (k, s), 0, W)], "nm"
+
+    def weight(q, s, j, i):
+        offs, fk = listed("of", s, j, i)
+        out, ok = wplace(s, j, i)
+        gather(q, out, ok, T["tb" + s][:], [("tb%s0" % s, 0, TW), ("tb%s1" % s, 0, TW), ("tz" + s, 0, 16)], offs, fk, 0.25)
+
+    def fetch(q, k, s, i):
+        win, wk, ln = window(k, s)
+        offs, fk = listed(ln, s, 0, i)
+        out, ok = term(s, 0, i)
+        gather(q, out, ok, win, wk, offs, fk)
+
+    def fused(k, s, j, i):
+        win, wk, ln = window(k, s)
+        offs, fk = listed(ln, s, j, i)
+        out, ok = term(s, j, i)
+        wv, wkey = wplace(s, j, i)
+        op("v", lambda: vec.tensor_tensor(out, win.indirect(offs), wv, A.mult), wk + fk + [wkey], [ok])
+
+    def scan(s, i):
+        a, b = CH[i]
+        op("v", lambda: vec.tensor_tensor_scan(T["Q" + s][:, 2 * a:2 * b], T["D0" + s][:, 2 * a:2 * b],
+                                               T["D1" + s][:, 2 * a:2 * b], 0.0, A.mult, A.add),
+           [("Dz" + s, a, b), ("Dw" + s, a, b), ("D1%s0" % s, a, b), ("D1%s1" % s, a, b)], [("Q" + s, a, b)])
+
+    def pe_x(s, i, b0):
+        a, b = CH[i]
+        si = STREAMS.index(s)
+        mm(b0 + i, 0, b - a, T.DD[half[si], :], T.Wx[half[si], a:b], True, False, [("DD%d" % si, 0, 128), ("Wx", a, b)])
+
+    def pe_term(s, j, i, b0, stop):
+        a, b = CH[i]
+        src, key = term(s, j, i)
+        mm(b0 + i, 0, b - a, T.SF[:], src, False, stop, [("SF", 0, 128), key])
+
+    def pe_q(s, i, b0):
+        a, b = CH[i]
+        mm(b0 + i, 0, b - a, T.SF[:], T["Q" + s][:, 2 * a + 1:2 * b:2], False, True, [("SF", 0, 128), ("Q" + s, a, b)])
+
+    def done(q, k, s, i, b0):
+        a, b = CH[i]
+        evict(q, "W%d%s" % (k + 1, s) if k < 4 else "Y" + s, a, b0 + i, 0, b - a, relu=True)
+
+    waiting = {x: list(plans[x][2][core]) for x in LATER}
+
+    def copies(q, x, n, near=False):
+        for ent in [e for e in waiting[x] if not near or e[0] in (0, 1, 2)][:n]:
+            waiting[x].remove(ent)
+            col = E + ent[1] * S
+            for h in range(2):
+                out, src = T["W" + x][half[h], col + SH:col + S], T["W" + x][half[1 - h], col:col + SH]
+                op(q, (lambda: vec.tensor_copy(out, src)) if q == "v" else (lambda: act.activation(out, src, ACT.Copy)),
+                   [("W" + x, col, col + SH)], [("W" + x, col + SH + h * HP, col + SH + (h + 1) * HP)])
+
+    def swap(x):
+        for j, (_, tt, _) in enumerate(waiting[x]):
+            col = E + tt * S
+            mm(4 + j % 4, 0, SH, T.SW[:], T["W" + x][:, col:col + SH], True, True, [("SW", 0, 128), ("W" + x, col, col + SH)])
+            evict("v", "W" + x, col + SH, 4 + j % 4, 0, SH)
+
+    meta(1)
+    turn_meta(1)
+    meta(3)
+    turn_meta(3)
+    meta(0)
     offsets(1)
-    first(1, 0)
-    first(1, 1)
-    for c in range(PE_FIRST[0], F):
-        v_add(0, c, c == F - 1)
-    first(1, 2)
-    if PE_FIRST[1] <= 2:
-        v_add(1, 2, False)
-    first(1, 3)
-    v_add(1, 3, True)
-    exchange(2, "SM", True)
-    keep_own(2)
+    turn_meta(0)
+    meta(2)
+    turn_meta(2)
+    offset_lists(1, 0)
+    offsets(0)
+    offset_lists(0, 0)
+    weight("a", "a", 1, 0)
+    for j, tt in enumerate(late):
+        col, bank = E + tt * S, 3 - j % 3
+        mm(bank, 0, S, T.SB[:], T.Wx[:, col:col + S], True, True, [("SB", 0, 128), ("Wx", col, col + S)])
+        evict("av"[j % 2], "Wx", W + col, bank, 0, S)
 
-    for u in range(2):
-        for c in range(F):
-            a = (u * F + c) * H
-            gather("av"[c % 2], T.wt[:, a:a + H], ("wt", a, a + H), T.tabw[:], ("tabw", 0, D * D + 16),
-                   T.offu[:, a // 16:(a + H) // 16], ("offu", a // 16, (a + H) // 16), scale=0.25)
-            if c < 3:
-                mm(2 + u * 3 + c, 0, H, IB, T.wt[:, a:a + H], True, True, [IBK, ("wt", a, a + H)])
+    def first(s, j, i, b0):
+        if j == 1:
+            pe_x(s, i, b0)
+        fused(1, s, j, i)
+        pe_term(s, j, i, b0, j == 0)
 
-    for k in range(2, 5):
-        wn = "W%d" % k
-        final = k == 4
-        pe_x(0)
-        pe_x(1)
-        for u, c in ((0, 0), (0, 1), (0, 2), (1, 0), (1, 1), (1, 2)):
-            a, b, offs, fk = term(u, c)
-            gather("a", T.GB[:, a:b], ("GB", a, b), T[wn][:], (wn, 0, W), offs, fk)
+    for j in (1, 0):
+        for i in NCH:
+            if (j, i) != (1, 0):
+                weight("a", "a", j, i)
+            first("a", j, i, 0)
+        offset_lists(j, 1)
+    for si, s in enumerate(STREAMS):
+        for h in range(2):
+            op("v", lambda: vec.tensor_copy(T["snd" + s][half[h], :], T.sndi[half[si], :, h * 8:(h + 1) * 8]),
+               [("sndi", 0, 112)], [("snd%s%d" % (s, h), 0, 56)])
+    for i in NCH[:2]:
+        weight("a", "b", 1, i)
+        first("b", 1, i, 4)
+    for i in NCH:
+        done("a", 1, "a", i, 0)
+    exchange("2a", "va")
+    for j in (1, 0):
+        for i in NCH[2 * j:]:
+            weight("a", "b", j, i)
+            first("b", j, i, 4)
+    later_lists()
+    for i in NCH:
+        done("a", 1, "b", i, 4)
+    copies("v", "2a", NCOPY)
+    exchange("2b", "a")
 
-        def fused(u):
-            a, b, offs, fk = term(u, 3)
-            op("v", lambda: vec.tensor_tensor(T.P[:, a:b], T[wn][:].indirect(offs), T.wt[:, a:b], A.mult),
-               [(wn, 0, W), fk, ("wt", a, b)], [("P", a, b)])
+    for x, nxt in zip(LATER, LATER[1:] + [None]):
+        k, s = int(x[0]), x[1]
+        si = STREAMS.index(s)
 
-        def mul(u, c):
-            a, bank = (u * F + c) * H, 2 + u * 3 + c
-            op("v", lambda: vec.tensor_tensor(T.P[:, a:a + H], pb[bank][:], T.GB[:, a:a + H], A.mult),
-               [("pb%d" % bank, 0, H), ("GB", a, a + H)], [("P", a, a + H)])
-        n0, n1 = PE_LATER
-        fused(0)
-        pe_add(0, 3, n0 == 1)
-        mul(0, 0)
-        if n0 >= 2:
-            pe_add(0, 0, n0 == 2)
-        fused(1)
-        mul(0, 1)
-        if n0 >= 3:
-            pe_add(0, 1, True)
-        pe_add(1, 3, n1 == 1)
-        mul(0, 2)
-        mul(1, 0)
-        if n1 >= 2:
-            pe_add(1, 0, n1 == 2)
-        for c in range(n0 - 1, 3):
-            v_add(0, c, c == 2)
-        if final:
-            op("a", lambda: act.activation(T.YB[:, 0:H], T.SM[:, 0:H], ACT.Relu), [("SM", 0, H)], [("YB", 0, H)])
-            dma("s", T.y[:, 0:H], T.YB[:, 0:H], [("YB", 0, H)], [])
-        mul(1, 1)
-        if n1 >= 3:
-            pe_add(1, 1, True)
-        for c in range(n1 - 1, 2):
-            v_add(1, c, False)
-        mul(1, 2)
-        if not final:
-            v_add(1, 2, True)
-            exchange(k + 1, "SM", True)
-            keep_own(k + 1)
-        else:
-            v_add(1, 2, True, parts=2)
-            m = H + H // 2
-            op("a", lambda: act.activation(T.YB[:, H:m], T.SM[:, H:m], ACT.Relu), [("SM", H, m)], [("YB", H, m)])
-            op("v", lambda: vec.tensor_scalar(T.YB[:, m:E], T.SM[:, m:E], 0.0, None, A.max), [("SM", m, E)], [("YB", m, E)])
-            dma("a", T.y[:, H:m], T.YB[:, H:m], [("YB", H, m)], [])
-            dma("s", T.y[:, m:E], T.YB[:, m:E], [("YB", m, E)], [])
+        def finish(i):
+            done("a", k, s, i, 0)
+            if k == 4 and i in (1, 3):
+                a, b = CH[i - 1][0], CH[i][1]
+                dma("s", T.y[half[si], a:b], T["Y" + s][half[0], a:b], [("Y" + s, a, b)], [])
+            if nxt:
+                copies("a", nxt, EARLY[i], True)
+        swap(x)
+        for i in NCH[NB:]:
+            fetch("a", k, s, i)
+        for i in NCH[:NB]:
+            pe_x(s, i, 0)
+            for j in (1, 0):
+                fused(k, s, j, i)
+                pe_term(s, j, i, 0, j == 0)
+            finish(i)
+        fused(k, s, 1, NB)
+        for i in NCH[NB:]:
+            if i + 1 in NCH:
+                fused(k, s, 1, i + 1)
+            scan(s, i)
+            pe_x(s, i, 0)
+            pe_q(s, i, 0)
+            finish(i)
+        if nxt:
+            copies("v", nxt, NCOPY)
+        if k < 4:
+            exchange(str(k + 1) + s, WHO_M)
 
     for sem in sorted(total):
         g.wait_ge(T.sem[sem], total[sem])

@@ -10,29 +10,29 @@ SH = S // 2
 HP = 64
 TW = D * D + 16
 STREAMS = "ab"
-CH = ((0, 384), (384, 704), (704, 896), (896, 1024))
+CH = ((0, 416), (416, 736), (736, 928), (928, 1024))
 LATER = [str(k) + s for k in range(2, 5) for s in STREAMS]
 NODE = 2.0 ** -9
 ROUND64 = 1.5 * 2.0 ** 29
-GM_A = 576
+GM_A = (544, 512, 640, 512)
 
-PLAN_X = (("B|B", "A|n", "A|nn"), (("C|B", "C|n", "A|nn"), ("C|B", "C|n", "A|nn")))
-PLAN_M = (("A|B", "A|n", "A|nn"), (("C|B", "C|B", "n|nn"), ("C|B", "C|B", "n|nn")))
+PLAN_X = ("B| |B A|n A|nn", "B| |B A|n A|nn", "C| |B C|n C|nn", "C| |B C|n C|nn")
+PLAN_M = ("A|B A|n A|nn", "A|B A|n A|nn", "C|B C|n C|nn", "C|B C|B n|nn")
 X_EARLY = 2
-LATE = 3
-WHO_M = "avaaaaa"
-EARLY = (0, 0, 0, 0)
-NCOPY = 2
-NB = 1
+LATE = 4
+WHO_A, WHO_M = "a2 v2 v3", "a2 a2 a3"
+EARLY = (1, 1, 0, 0)
+LAST_V = 3
+HELD = 2
 
 SCRATCH = {
     "CI": ("sbuf", [128, 512], "int32"), "CB": ("sbuf", [128, 512], "bfloat16"),
     "RL": ("sbuf", [128, 512], "bfloat16"), "ZZ": ("sbuf", [128, 144], "bfloat16"),
     "ZI": ("sbuf", [128, 160], "bfloat16"), "I4": ("sbuf", [128, 128], "bfloat16"),
     "IF": ("sbuf", [128, 128], "float32"), "DD": ("sbuf", [128, 128], "bfloat16"),
-    "SF": ("sbuf", [128, 128], "float32"), "SW": ("sbuf", [128, 128], "float32"),
-    "SB": ("sbuf", [128, 128], "bfloat16"),
+    "SF": ("sbuf", [128, 128], "float32"), "SB": ("sbuf", [128, 128], "bfloat16"),
     "sndi": ("sbuf", [128, NR - 1, 16], "int32"), "sndu": ("sbuf", [128, 112], "uint16"),
+    "sndp": ("sbuf", [128, NR - 1, 16], "int32"),
     "nbi": ("sbuf", [128, 256], "int32"), "nbu": ("sbuf", [128, 256], "uint16"),
     "f1": ("sbuf", [128, 128], "int32"), "f2": ("sbuf", [128, 128], "int32"), "f3": ("sbuf", [128, 128], "int32"),
     "rt": ("sbuf", [128, 256], "bfloat16"), "et": ("sbuf", [128, 256], "bfloat16"),
@@ -41,7 +41,7 @@ SCRATCH = {
     "C0": ("sbuf", [128, (NR - 1) * SQ], "bfloat16"), "L0": ("sbuf", [128, (NR - 1) * SQ], "bfloat16"),
     "W0": ("sbuf", [128, W], "bfloat16"), "Wx": ("sbuf", [128, 2 * W], "bfloat16"),
     "B0": ("sbuf", [128, NS], "bfloat16"), "Bx": ("sbuf", [128, NS], "bfloat16"),
-    "GM": ("sbuf", [128, F * E], "bfloat16"),
+    "GM": ("sbuf", [128, F * E], "bfloat16"), "G1": ("sbuf", [128, E], "float32"),
 }
 for _s in STREAMS:
     SCRATCH["snd" + _s] = ("sbuf", [128, 56], "uint16")
@@ -96,10 +96,10 @@ def small_plan(T, topo, c):
     return list(zip(fa, split([lo], len(fa)))), list(zip(ne, split([hi], len(ne))))
 
 
-def make_plan(T, topo, plan):
+def make_plan(T, topo, plan, back=0):
     cores = list(T.cores)
     n = len(cores)
-    calls, relay, arr = {}, {}, {c: [] for c in cores}
+    calls, relay, arr, handed = {}, {}, {c: [] for c in cores}, []
     for r, c in enumerate(cores):
         near, far, i, lo, hi = sides(T, topo, c)
         over = [z for z in topo.cores_of(c) if topo.die(z) != topo.die(c) and z not in cores]
@@ -107,36 +107,42 @@ def make_plan(T, topo, plan):
                   and topo.may_write(z, far[0])]
         beyond.sort(key=lambda z: topo.die(z) != topo.die(c))
         owners = [a for a in near if topo.may_write(a, beyond[0])]
-        mine = plan[1][owners.index(c) % len(plan[1])] if c in owners else plan[0]
-        used = {"far": 0, "n": 0, "B": 0, "C": 0}
+        mine = plan[sorted(near, key=lambda a: a in owners).index(c)].split()
+        if back:
+            over.reverse()
+        used = {"far": 0, "n": 0}
         calls[c] = []
         for j, call in enumerate(mine):
             out = []
             for ways, engines in zip(call.split("|"), (lo, hi)):
-                for way, engs in zip(ways, split([engines], len(ways))):
-                    z = None
+                for way, engs in zip(ways, split([engines], max(1, len(ways)))):
                     if way == "n":
                         used["n"] += 1
                         d = near[(i + used["n"]) % len(near)]
                     else:
                         d = far[(i + used["far"]) % len(far)]
                         used["far"] += 1
-                    if way == "B":
-                        z = over[(i + 2 * used["B"]) % len(over)]
-                        used["B"] += 1
-                    elif way == "C":
-                        z = beyond[(owners.index(c) + len(owners) * used["C"]) % len(beyond)]
-                        used["C"] += 1
                     t = (cores.index(d) - r) % n
-                    ent = {"t": t, "to": d, "engs": engs, "tt": n - t - 1, "z": z}
-                    if z is None:
+                    ent = {"t": t, "to": d, "engs": engs, "tt": n - t - 1, "way": way, "key": (j, i), "next": None}
+                    out.append(ent)
+                    if way in "nA":
                         arr[d].append((j + (0.5 if way == "A" else 0), n - t - 1, len(engs)))
                     else:
-                        ent.update({"to": z, "dst": d, "key": (j, r)})
-                        relay.setdefault(z, []).append(ent)
-                        arr[d].append((j + LATE, n - t - 1, len(topo.engines(z, d))))
-                    out.append(ent)
+                        across = [z for z in beyond if topo.die(z) != topo.die(c)]
+                        stops = {"B": [over], "C": [beyond],
+                                 "D": [[z for z in over if topo.may_write(z, across[0])], across]}[way]
+                        handed.append((ent, stops))
             calls[c].append(out)
+    for ent, stops in sorted(handed, key=lambda h: (-len(h[1]), h[0]["key"])):
+        d = ent["to"]
+        for hop, choice in enumerate(stops):
+            z = min(choice, key=lambda z: len(relay.get(z, [])))
+            nxt = {"to": d, "tt": ent["tt"], "key": (ent["key"][0] + hop * LATE, ent["key"][1]), "next": None,
+                   "count": len(ent["engs"]) if hop == 0 else len(topo.engines(at, z))}
+            relay.setdefault(z, []).append(nxt)
+            ent["to"], ent["next"] = z, nxt
+            ent, at = nxt, z
+        arr[d].append((ent["key"][0] + LATE, ent["tt"], len(topo.engines(at, d))))
     for z in relay:
         relay[z].sort(key=lambda e: e["key"])
         for j, e in enumerate(relay[z]):
@@ -146,11 +152,13 @@ def make_plan(T, topo, plan):
     return calls, relay, arr
 
 
-def landing(T, x, tt):
-    col = E + tt * S
-    if x == "x":
-        return T.Wx[:, col:col + S], "arx_%d" % tt
-    return T["W" + x][:, col:col + SH], "ar%s_%d" % (x, tt)
+def landing(T, x, e):
+    n = S if x == "x" else SH
+    if e["next"]:
+        j = e["next"]["slot"]
+        return T["B" + x][:, j * n:(j + 1) * n], "rl%s_%d" % (x, j)
+    col = E + e["tt"] * S
+    return T["W" + x][:, col:col + n], "ar%s_%d" % (x, e["tt"])
 
 
 def helper_program(g, core, T, topo, plans):
@@ -159,21 +167,21 @@ def helper_program(g, core, T, topo, plans):
         n = S if x == "x" else SH
         for e in plans[x][1].get(core, []):
             j = e["slot"]
-            g.wait_ge(T.sem["rl%s_%d" % (x, j)], len(e["engs"]))
-            rid, pid, _ = topo.addr(e["dst"])
-            dst, sem = landing(T, x, e["tt"])
+            g.wait_ge(T.sem["rl%s_%d" % (x, j)], e["count"])
+            rid, pid, _ = topo.addr(e["to"])
+            dst, sem = landing(T, x, e)
             g.remote_dma(dst, T["B" + x][:, j * n:(j + 1) * n], T.sem[sem], T.sem.sent, pid, rid,
-                         topo.mask(core, e["dst"]))
-            sent += len(topo.engines(core, e["dst"]))
+                         topo.mask(core, e["to"]))
+            sent += len(topo.engines(core, e["to"]))
     if sent:
         g.wait_ge(T.sem.sent, sent)
 
 
 def rank_program(g, core, T, topo):
     plans = {"x": make_plan(T, topo, PLAN_X)}
-    plan_m = make_plan(T, topo, PLAN_M)
+    by_stream = {s: make_plan(T, topo, PLAN_M, si) for si, s in enumerate(STREAMS)}
     for x in LATER:
-        plans[x] = plan_m
+        plans[x] = by_stream[x[1]]
     rank = T.rank_of(core)
     if rank is None:
         helper_program(g, core, T, topo, plans)
@@ -261,12 +269,9 @@ def rank_program(g, core, T, topo):
         op(q, fn, wkeys + fkeys, [okey])
 
     def piece(q, x, t):
-        if x in ("0", "x"):
-            a, n, offs, fk = (t - 1) * S, S, T.sndu[:, (t - 1) * 16:t * 16], [("sndu", 0, 112)]
-        else:
-            a, n, offs = (t - 1) * SH, SH, T["snd" + x[1]][:, (t - 1) * 8:t * 8]
-            fk = [("snd%s%d" % (x[1], h), 0, 56) for h in range(2)]
-        gather(q, T["B" + x][:, a:a + n], ("B" + x, a, a + n), T["W" + x][:, 0:E], [("W" + x, 0, E)], offs, fk)
+        a = (t - 1) * S
+        gather(q, T["B" + x][:, a:a + S], ("B" + x, a, a + S), T["W" + x][:, 0:E], [("W" + x, 0, E)],
+               T.sndu[:, (t - 1) * 16:t * 16], [("sndu", 0, 112)])
 
     def send(trs, local):
         order("g", [x[4] for x in trs], [])
@@ -287,26 +292,30 @@ def rank_program(g, core, T, topo):
         for call in plans[x][0][core][lo:hi]:
             trs = []
             for e in call:
-                a = (e["t"] - 1) * n
-                if e["z"] is None:
-                    dst, sem = landing(T, x, e["tt"])
-                else:
-                    dst, sem = B[:, e["slot"] * n:(e["slot"] + 1) * n], "rl%s_%d" % (x, e["slot"])
+                a = (e["t"] - 1 if x == "x" else turns.index(e["t"])) * n
+                dst, sem = landing(T, x, e)
                 trs.append((e["to"], e["engs"], sem, B[:, a:a + n], ("B" + x, a, a + n), dst))
             send(trs, "sentx" if x == "x" else "sent")
 
+    turns = [e["t"] for call in plans[LATER[0]][0][core] for e in call]
+
     def exchange(x, who):
-        pieces(x, who)
+        lo = 0
+        for q, n in who.split():
+            hi = lo + int(n)
+            gather(q, T["B" + x][:, lo * SH:hi * SH], ("B" + x, lo * SH, hi * SH), T["W" + x][:, 0:E], [("W" + x, 0, E)],
+                   T["snd" + x[1]][:, lo * 8:hi * 8], [("snd%s%d" % (x[1], h), 0, 56) for h in range(2)])
+            lo = hi
         calls(x)
         for _, tt, cnt in plans[x][2][core]:
-            sem = landing(T, x, tt)[1]
+            sem = "ar%s_%d" % (x, tt)
             total[sem] = cnt
             hist["W" + x].append((E + tt * S, E + tt * S + SH, True, "r", (sem, cnt)))
 
     dma("s", T.CI[32:64, 0:256], T.srcs[:], [], [("CI1", 0, 256)])
     dma("a", T.sndi[:], T.snd[:], [], [("sndi", 0, 112)])
-    dma("a", T.CI[0:32, 0:256], T.dirs[:], [], [("CI0", 0, 256)])
-    dma("a", T.Wx[:, 0:E], T.x[:], [], [("Wx", 0, E)])
+    dma("s", T.CI[0:32, 0:256], T.dirs[:], [], [("CI0", 0, 256)])
+    dma("s", T.Wx[:, 0:E], T.x[:], [], [("Wx", 0, E)])
     dma("s", T.CI[32:64, 256:512], T.dsts[:], [], [("CI1", 256, 512)])
     dma("s", T.CI[0:32, 256:512], T.dirs[:], [], [("CI0", 256, 512)])
     dma("s", T.nbi[:], T.nb[:], [], [("nbi", 0, 256)])
@@ -329,8 +338,8 @@ def rank_program(g, core, T, topo):
     def sel(name, n, pattern, cmp, base, cm, fill=0.0):
         op("g", lambda: g.affine_select(T[name][:], T[name][:], pattern, cmp, fill, base, cm), [(name, 0, n)], [(name, 0, n)])
     sel("ZI", 160, [[-1, 160]], A.is_equal, 16, 1)
-    sel("RL", 512, [[-1, 4], [-4, 8], [-32, 16]], A.is_equal, 0, 1)
     sel("ZZ", 144, [[-16, 9], [1000, 16]], A.is_ge, -15000, 1)
+    sel("RL", 512, [[-1, 4], [-4, 8], [-32, 16]], A.is_equal, 0, 1)
     sel("ZZ", 144, [[16, 9], [0, 16]], A.is_ge, 2, -1)
     sel("ZZ", 144, [[-16, 9], [1000, 16]], A.not_equal, -15000, 1, float(D))
     op("a", lambda: act.activation(T.IF[:], IB, ACT.Copy), [IBK], [("IF", 0, 128)])
@@ -341,44 +350,63 @@ def rank_program(g, core, T, topo):
                [IBK], [("DD%d" % h, m * HP, (m + 1) * HP)])
     DDK = [("DD0", 0, 128), ("DD1", 0, 128)]
     op("a", lambda: act.activation(T.SF[:], T.DD[:], ACT.Copy), DDK, [("SF", 0, 128)])
-    op("v", lambda: vec.tensor_tensor(T.SW[:], T.DD[:], IB, A.subtract), DDK + [IBK], [("SW", 0, 128)])
-    op("a", lambda: act.activation(T.SB[:], T.SW[:], ACT.Copy), [("SW", 0, 128)], [("SB", 0, 128)])
 
-    def rows(lo, b0, wname, who):
+    def rounded(lo):
         hi = lo + 256
         op("v", lambda: vec.tensor_copy(T.CB[0:64, lo:hi], T.CI[0:64, lo:hi]),
            [("CI0", lo, hi), ("CI1", lo, hi)], [("CB0", lo, hi)])
+
+    def rest(lo):
+        hi = lo + 256
         op("v", lambda: vec.tensor_tensor(T.CB[64:96, lo:hi], T.CI[32:64, lo:hi], T.CB[32:64, lo:hi], A.subtract),
            [("CI1", lo, hi), ("CB0", lo, hi)], [("CB1", lo, hi)])
+
+    def rows(lo, b0):
+        hi = lo + 256
         for q in range(4):
             mm(b0 + q // 2, (q % 2) * 256, (q % 2) * 256 + 256, T.RL[0:96, q * 128:(q + 1) * 128], T.CB[0:96, lo:hi],
                True, True, [("RL", 0, 512), ("CB0", lo, hi), ("CB1", lo, hi)])
-        evict(who[0], wname, 0, b0, 0, H)
-        evict(who[1], wname, H, b0 + 1, 0, H)
 
     op("v", lambda: vec.tensor_copy(T.sndu[:], T.sndi[:]), [("sndi", 0, 112)], [("sndu", 0, 112)])
     pieces("x", "a", 0, X_EARLY)
-    calls("x", 0, 1)
-    rows(0, 0, "W0", "va")
+    calls("x", 0, X_EARLY)
+    rounded(0)
+    op("v", lambda: vec.tensor_tensor(T.SB[:], T.DD[:], IB, A.subtract), DDK + [IBK], [("SB", 0, 128)])
+    rest(0)
+    rows(0, 0)
+    rounded(256)
+    evict("v", "W0", 0, 0, 0, H)
+    evict("a", "W0", H, 1, 0, H)
+    rest(256)
+    rows(256, 6)
 
     cores = list(T.cores)
     mine = small_plan(T, topo, core)
-    for part, sem, bank0 in ((mine[0], "mfar", 2), (mine[1], "mnear", 4)):
+
+    def small(part, sem, bank0, step):
         ts = [(cores.index(d) - rank) % NR for d, _ in part]
         c0 = 0 if sem == "mfar" else len(mine[0]) * SQ
         hf = (len(ts) + 1) // 2
         turn = sorted(range(len(ts)), key=lambda j: (j % hf, j))
-        for j in turn:
-            piece("va"[j // hf], "0", ts[j])
-        for j in turn:
-            for q in range(4):
-                a = (ts[j] - 1) * S + q * SQ
-                mm(bank0 + j // hf, (j % hf) * SQ, (j % hf + 1) * SQ, T.ZI[:, 16 - 4 * q:144 - 4 * q],
-                   T.B0[:, a:a + SQ], q == 0, q == 3, [IBK, ("B0", a, a + SQ)])
+        if step == "fold":
+            for j in turn:
+                piece("va"[j // hf], "0", ts[j])
+            for j in turn:
+                for q in range(4):
+                    a = (ts[j] - 1) * S + q * SQ
+                    mm(bank0 + j // hf, (j % hf) * SQ, (j % hf + 1) * SQ, T.ZI[:, 16 - 4 * q:144 - 4 * q],
+                       T.B0[:, a:a + SQ], q == 0, q == 3, [IBK, ("B0", a, a + SQ)])
+            return
         evict("v", "C0", c0, bank0, 0, hf * SQ)
         evict("a", "C0", c0 + hf * SQ, bank0 + 1, 0, (len(ts) - hf) * SQ)
         send([(d, engs, sem, T.C0[:, c0 + j * SQ:c0 + (j + 1) * SQ], ("C0", c0 + j * SQ, c0 + (j + 1) * SQ),
                T.L0[:, (NR - ts[j] - 1) * SQ:(NR - ts[j]) * SQ]) for j, (d, engs) in enumerate(part)], "sentx")
+    small(mine[0], "mfar", 2, "fold")
+    small(mine[1], "mnear", 4, "fold")
+    pieces("x", "a", X_EARLY, X_EARLY + 1)
+    small(mine[0], "mfar", 2, "send")
+    pieces("x", "va", X_EARLY + 1, X_EARLY + 3)
+    small(mine[1], "mnear", 4, "send")
     landed = {"mfar": [], "mnear": []}
     for q0 in cores:
         for part, sem in zip(small_plan(T, topo, q0), ("mfar", "mnear")):
@@ -389,16 +417,17 @@ def rank_program(g, core, T, topo):
     for sem in landed:
         for tt in landed[sem]:
             hist.setdefault("L0", []).append((tt * SQ, tt * SQ + SQ, True, "r", (sem, total[sem])))
-    pieces("x", "av", X_EARLY)
-    calls("x", 1)
+    pieces("x", "va", X_EARLY + 3)
+    calls("x", X_EARLY)
     for _, tt, cnt in plans["x"][2][core]:
         total["arx_%d" % tt] = cnt
         hist["Wx"].append((E + tt * S, E + tt * S + S, True, "r", ("arx_%d" % tt, cnt)))
 
-    rows(256, 6, "DW", "av")
+    evict("a", "DW", 0, 6, 0, H)
+    evict("v", "DW", H, 7, 0, H)
     op("v", lambda: vec.tensor_copy(T.nbu[:], T.nbi[:]), [("nbi", 0, 256)], [("nbu", 0, 256)])
-    load_tab(1, [("nbu", 0, 256)])
-    late = [tt for when, tt, _ in plans["x"][2][core] if when >= LATE]
+    when = {tt: w for w, tt, _ in plans["x"][2][core]}
+    late = [tt for _, tt, _ in plans["x"][2][core][-2:]]
     runs = []
     for tt in range(NR - 1):
         if tt in late:
@@ -407,10 +436,11 @@ def rank_program(g, core, T, topo):
             runs[-1][1] += 1
         else:
             runs.append([tt, tt + 1])
-    for lo, hi in runs:
+    for lo, hi in sorted(runs, key=lambda r: max(when[tt] for tt in range(*r))):
         a, b = E + lo * S, E + hi * S
         for h in range(2):
             dma("s", T.Wx[half[h], W + a:W + b], T.Wx[half[1 - h], a:b], [("Wx", a, b)], [("Vx%d" % h, a, b)])
+    load_tab(1, [])
     for si, s in enumerate(STREAMS):
         for h in range(2):
             op("v", lambda: vec.tensor_scalar(T["nx" + s][half[h], :], T.nbi[half[si], h * 128:(h + 1) * 128],
@@ -420,6 +450,12 @@ def rank_program(g, core, T, topo):
         mm(0, 0, 64, T.ZZ[:, 15 - h:143 - h], T.DW[:, h:E:16], h == 0, h == 15, [("ZZ", 0, 144), ("DW", 0, E)])
     op("v", lambda: vec.tensor_scalar(T.ro[:], pb[0][:, 0:64], ROUND64, ROUND64, A.add, A.subtract),
        [("pb0", 0, 64)], [("ro", 0, 64)])
+    lo = 0
+    for hi in range(1, NR):
+        if hi == NR - 1 or turns[hi] != turns[hi - 1] + 1:
+            op("v", lambda: vec.tensor_copy(T.sndp[:, lo:hi, :], T.sndi[:, turns[lo] - 1:turns[hi - 1], :]),
+               [("sndi", 0, 112)], [("sndp", lo, hi)])
+            lo = hi
     op("v", lambda: vec.tensor_tensor(T.dL[:], T.ro[:], pb[0][:, 0:64], A.subtract), [("pb0", 0, 64), ("ro", 0, 64)],
        [("dL", 0, 64)])
     for u in range(2):
@@ -427,18 +463,20 @@ def rank_program(g, core, T, topo):
            [("bL", u * 64, u * 64 + 64)])
 
     nb0 = 0
-    for sem in ("mnear", "mfar"):
+    for sem in ("mfar", "mnear"):
         for j, tt in enumerate(landed[sem]):
             bank = 1 + nb0 + j
             for q in range(4):
                 mm(bank, q * SQ, (q + 1) * SQ, T.ZI[:, 16 + 4 * q:144 + 4 * q], T.L0[:, tt * SQ:(tt + 1) * SQ], True, True,
                    [IBK, ("L0", tt * SQ, (tt + 1) * SQ)])
             evict("av"[j % 2], "W0", E + tt * S, bank, 0, S)
-        nb0 = 3
+        nb0 += len(landed[sem])
 
-    def meta(c):
-        for q, a, b in (("a", c * E, c * E + GM_A), ("v", c * E + GM_A, (c + 1) * E)):
-            gather(q, T.GM[:, a:b], ("GM", a, b), T.W0[:], [("W0", 0, W)], T.nbu[:, a // 16:b // 16], [("nbu", 0, 256)])
+    def meta(q, c, part=None):
+        a, b = (c * E, c * E + GM_A[c]) if q == "a" else (c * E + GM_A[c], (c + 1) * E)
+        if part is not None:
+            a, b = ((a, (a + b) // 2), ((a + b) // 2, b))[part]
+        gather(q, T.GM[:, a:b], ("GM", a, b), T.W0[:], [("W0", 0, W)], T.nbu[:, a // 16:b // 16], [("nbu", 0, 256)])
 
     def turn_meta(c):
         lo = (c // 2) * 64
@@ -447,11 +485,18 @@ def rank_program(g, core, T, topo):
             mm(4 + c % 2, lo, lo + 64, T.ZZ[:, 15 - h:143 - h], T.GM[:, c * E + h:(c + 1) * E:16],
                False, h == 15, [("ZZ", 0, 144), ("GM", c * E, (c + 1) * E)])
 
+    def rounded_z(j):
+        a, b = j * 128, j * 128 + 128
+        op("v", lambda: vec.tensor_scalar(T.rt[:, a:b], pb[4 + j][:, 0:128], ROUND64, ROUND64, A.add, A.subtract),
+           [("pb%d" % (4 + j), 0, 128)], [("rt", a, b)])
+
+    def reverse(j):
+        a, b = j * 128, j * 128 + 128
+        op("v", lambda: vec.tensor_tensor(T.et[:, a:b], pb[4 + j][:, 0:128], T.rt[:, a:b], A.is_equal),
+           [("pb%d" % (4 + j), 0, 128), ("rt", a, b)], [("et", a, b)])
+
     def offsets(j):
         a, b = j * 128, j * 128 + 128
-        z, zk = pb[4 + j][:, 0:128], ("pb%d" % (4 + j), 0, 128)
-        op("v", lambda: vec.tensor_scalar(T.rt[:, a:b], z, ROUND64, ROUND64, A.add, A.subtract), [zk], [("rt", a, b)])
-        op("v", lambda: vec.tensor_tensor(T.et[:, a:b], z, T.rt[:, a:b], A.is_equal), [zk, ("rt", a, b)], [("et", a, b)])
         mm(6 + j, 0, 128, IB, T.bL[:], True, False, [IBK, ("bL", 0, 128)])
         mm(6 + j, 0, 128, IB, T.rt[:, a:b], False, False, [IBK, ("rt", a, b)])
         mm(6 + j, 0, 128, T.I4[:], T.et[:, a:b], False, True, [("I4", 0, 128), ("et", a, b)])
@@ -475,19 +520,22 @@ def rank_program(g, core, T, topo):
         for si, s in enumerate(STREAMS):
             op("v", lambda: vec.tensor_copy(T["nm" + s][half[1], :], T.f2[half[si], :]), [("f2", 0, 128)], [("nm%s1" % s, 0, 128)])
 
+    def edges(i):
+        return CH[i] if isinstance(i, int) else (CH[i[0]][0], CH[i[-1]][1])
+
     def listed(name, s, j, i):
-        a, b = CH[i]
+        a, b = edges(i)
         lo, hi = j * 64 + a // 16, j * 64 + b // 16
         return T[name + s][:, lo:hi], [("%s%s%d" % (name, s, h), lo, hi) for h in range(2)]
 
     def wplace(s, j, i):
-        a, b = CH[i]
+        a, b = edges(i)
         if j == 0:
             return T["D0" + s][:, 2 * a + 1:2 * b:2], ("Dw" + s, a, b)
         return T["w1" + s][:, a:b], ("w1" + s, a, b)
 
     def term(s, j, i):
-        a, b = CH[i]
+        a, b = edges(i)
         return T["D1" + s][:, 2 * a + j:2 * b:2], ("D1%s%d" % (s, j), a, b)
 
     def window(k, s):
@@ -500,11 +548,23 @@ def rank_program(g, core, T, topo):
         out, ok = wplace(s, j, i)
         gather(q, out, ok, T["tb" + s][:], [("tb%s0" % s, 0, TW), ("tb%s1" % s, 0, TW), ("tz" + s, 0, 16)], offs, fk, 0.25)
 
-    def fetch(q, k, s, i):
+    def fetch(q, k, s, j, i):
         win, wk, ln = window(k, s)
-        offs, fk = listed(ln, s, 0, i)
-        out, ok = term(s, 0, i)
+        offs, fk = listed(ln, s, j, i)
+        a, b = CH[i]
+        out, ok = term(s, 0, i) if j == 0 else (T.G1[:, a:b], ("G1", a, b))
         gather(q, out, ok, win, wk, offs, fk)
+
+    def hold(s):
+        a, b = CH[HELD]
+        mm(6 + STREAMS.index(s), 0, b - a, IB, T["w1" + s][:, a:b], True, True, [IBK, ("w1" + s, a, b)])
+
+    def times(s, i):
+        a, b = CH[i]
+        bank, lo = 6 + STREAMS.index(s), 0
+        out, ok = term(s, 1, i)
+        op("v", lambda: vec.tensor_tensor(out, pb[bank][:, lo:lo + b - a], T.G1[:, a:b], A.mult),
+           [("pb%d" % bank, lo, lo + b - a), ("G1", a, b)], [ok])
 
     def fused(k, s, j, i):
         win, wk, ln = window(k, s)
@@ -539,70 +599,81 @@ def rank_program(g, core, T, topo):
 
     waiting = {x: list(plans[x][2][core]) for x in LATER}
 
-    def copies(q, x, n, near=False):
-        for ent in [e for e in waiting[x] if not near or e[0] in (0, 1, 2)][:n]:
+    def copies(who, x, n):
+        for ent in waiting[x][:n]:
             waiting[x].remove(ent)
             col = E + ent[1] * S
             for h in range(2):
+                q = who[h % len(who)]
                 out, src = T["W" + x][half[h], col + SH:col + S], T["W" + x][half[1 - h], col:col + SH]
                 op(q, (lambda: vec.tensor_copy(out, src)) if q == "v" else (lambda: act.activation(out, src, ACT.Copy)),
                    [("W" + x, col, col + SH)], [("W" + x, col + SH + h * HP, col + SH + (h + 1) * HP)])
 
-    def swap(x):
-        for j, (_, tt, _) in enumerate(waiting[x]):
-            col = E + tt * S
-            mm(4 + j % 4, 0, SH, T.SW[:], T["W" + x][:, col:col + SH], True, True, [("SW", 0, 128), ("W" + x, col, col + SH)])
-            evict("v", "W" + x, col + SH, 4 + j % 4, 0, SH)
+    def x_across(j, q):
+        col = E + late[j] * S
+        mm(3 - j, 0, S, T.SB[:], T.Wx[:, col:col + S], True, True, [("SB", 0, 128), ("Wx", col, col + S)])
+        evict(q, "Wx", W + col, 3 - j, 0, S)
 
-    meta(1)
-    turn_meta(1)
-    meta(3)
-    turn_meta(3)
-    meta(0)
+    for c in (1, 3, 0):
+        meta("a", c)
+        meta("v", c)
+        turn_meta(c)
+    meta("a", 2)
+    meta("v", 2, 0)
+    rounded_z(1)
+    meta("v", 2, 1)
+    reverse(1)
     offsets(1)
-    turn_meta(0)
-    meta(2)
     turn_meta(2)
-    offset_lists(1, 0)
-    offsets(0)
-    offset_lists(0, 0)
-    weight("a", "a", 1, 0)
-    for j, tt in enumerate(late):
-        col, bank = E + tt * S, 3 - j % 3
-        mm(bank, 0, S, T.SB[:], T.Wx[:, col:col + S], True, True, [("SB", 0, 128), ("Wx", col, col + S)])
-        evict("av"[j % 2], "Wx", W + col, bank, 0, S)
-
-    def first(s, j, i, b0):
-        if j == 1:
-            pe_x(s, i, b0)
-        fused(1, s, j, i)
-        pe_term(s, j, i, b0, j == 0)
-
-    for j in (1, 0):
-        for i in NCH:
-            if (j, i) != (1, 0):
-                weight("a", "a", j, i)
-            first("a", j, i, 0)
-        offset_lists(j, 1)
     for si, s in enumerate(STREAMS):
         for h in range(2):
-            op("v", lambda: vec.tensor_copy(T["snd" + s][half[h], :], T.sndi[half[si], :, h * 8:(h + 1) * 8]),
-               [("sndi", 0, 112)], [("snd%s%d" % (s, h), 0, 56)])
-    for i in NCH[:2]:
-        weight("a", "b", 1, i)
-        first("b", 1, i, 4)
+            op("v", lambda: vec.tensor_copy(T["snd" + s][half[h], :], T.sndp[half[si], :, h * 8:(h + 1) * 8]),
+               [("sndp", 0, NR - 1)], [("snd%s%d" % (s, h), 0, 56)])
+    offset_lists(1, 0)
+    weight("a", "a", 1, NCH[2:])
+    rounded_z(0)
+    x_across(0, "v")
+    reverse(0)
+    x_across(1, "a")
+    offsets(0)
+
+    def sums(s, j, span):
+        for i in span:
+            if j == 1:
+                pe_x(s, i, 4 * STREAMS.index(s))
+            pe_term(s, j, i, 4 * STREAMS.index(s), j == 0)
+
+    def first(s, j, span, weights=True, summed=True):
+        if weights:
+            weight("a", s, j, span)
+        fused(1, s, j, span)
+        if summed:
+            sums(s, j, span)
+
+    first("a", 1, NCH[2:], False)
+    offset_lists(0, 0)
+    first("a", 1, [1])
+    first("a", 1, [0])
+    offset_lists(1, 1)
+    for i in NCH:
+        first("a", 0, [i])
+    offset_lists(0, 1)
+    first("b", 1, [0])
+    first("b", 1, [1])
+    first("b", 1, NCH[2:], True, False)
     for i in NCH:
         done("a", 1, "a", i, 0)
-    exchange("2a", "va")
-    for j in (1, 0):
-        for i in NCH[2 * j:]:
-            weight("a", "b", j, i)
-            first("b", j, i, 4)
+    exchange("2a", WHO_A)
+    sums("b", 1, NCH[2:])
+    for span in ([0], [1], NCH[2:]):
+        first("b", 0, span)
     later_lists()
     for i in NCH:
         done("a", 1, "b", i, 4)
-    copies("v", "2a", NCOPY)
-    exchange("2b", "a")
+    for s in STREAMS:
+        hold(s)
+    copies("v", "2a", NR)
+    exchange("2b", WHO_M)
 
     for x, nxt in zip(LATER, LATER[1:] + [None]):
         k, s = int(x[0]), x[1]
@@ -613,27 +684,33 @@ def rank_program(g, core, T, topo):
             if k == 4 and i in (1, 3):
                 a, b = CH[i - 1][0], CH[i][1]
                 dma("s", T.y[half[si], a:b], T["Y" + s][half[0], a:b], [("Y" + s, a, b)], [])
-            if nxt:
-                copies("a", nxt, EARLY[i], True)
-        swap(x)
-        for i in NCH[NB:]:
-            fetch("a", k, s, i)
-        for i in NCH[:NB]:
+            if x == LATER[-2]:
+                copies("a", nxt, EARLY[i])
+        for i in NCH:
             pe_x(s, i, 0)
-            for j in (1, 0):
-                fused(k, s, j, i)
-                pe_term(s, j, i, 0, j == 0)
-            finish(i)
-        fused(k, s, 1, NB)
-        for i in NCH[NB:]:
-            if i + 1 in NCH:
-                fused(k, s, 1, i + 1)
+
+        def scanned(i):
             scan(s, i)
-            pe_x(s, i, 0)
             pe_q(s, i, 0)
             finish(i)
+        fetch("a", k, s, 1, HELD)
+        for i in NCH[1:]:
+            fetch("a", k, s, 0, i)
+        fused(k, s, 1, 0)
+        pe_term(s, 1, 0, 0, False)
+        fused(k, s, 1, 1)
+        fused(k, s, 0, 0)
+        pe_term(s, 0, 0, 0, True)
+        finish(0)
+        times(s, HELD)
+        scanned(1)
+        fused(k, s, 1, 3)
+        scanned(2)
+        scanned(3)
         if nxt:
-            copies("v", nxt, NCOPY)
+            copies("v", nxt, NR if nxt != LATER[-1] else LAST_V)
+        if nxt == LATER[-1]:
+            copies("va", nxt, NR)
         if k < 4:
             exchange(str(k + 1) + s, WHO_M)
 

from concourse.bass import DstId, RemoteDMATransfer
from concourse.mybir import AluOpType, ActivationFunctionType

E, S, D, F, V, NR, SIM = 1024, 256, 64, 4, 16384, 8, 64
W = E + (NR - 1) * S
NS = (NR - 1) * S
H = E // 2
SQ = S // 4
SH = S // 2
HP = 64
TW = D * D + 16
STREAMS = "ab"
CH = ((0, 416), (416, 736), (736, 928), (928, 1024))
LATER = [str(k) + s for k in range(2, 5) for s in STREAMS]
NODE = 2.0 ** -9
ROUND64 = 1.5 * 2.0 ** 29
GM_A = (544, 512, 640, 512)

PLAN_X = ("B| |B A|n A|nn", "B| |B A|n A|nn", "C| |B C|n C|nn", "C| |B C|n C|nn")
PLAN_M = ("A|B A|n A|nn", "A|B A|n A|nn", "C|B C|n C|nn", "C|B C|B n|nn")
X_EARLY = 2
LATE = 4
WHO_A, WHO_M = "a2 v2 v3", "a2 a2 a3"
EARLY = (1, 1, 0, 0)
LAST_V = 3
HELD = 2

SCRATCH = {
    "CI": ("sbuf", [128, 512], "int32"), "CB": ("sbuf", [128, 512], "bfloat16"),
    "RL": ("sbuf", [128, 512], "bfloat16"), "ZZ": ("sbuf", [128, 144], "bfloat16"),
    "ZI": ("sbuf", [128, 160], "bfloat16"), "I4": ("sbuf", [128, 128], "bfloat16"),
    "IF": ("sbuf", [128, 128], "float32"), "DD": ("sbuf", [128, 128], "bfloat16"),
    "SF": ("sbuf", [128, 128], "float32"), "SB": ("sbuf", [128, 128], "bfloat16"),
    "sndi": ("sbuf", [128, NR - 1, 16], "int32"), "sndu": ("sbuf", [128, 112], "uint16"),
    "sndp": ("sbuf", [128, NR - 1, 16], "int32"),
    "nbi": ("sbuf", [128, 256], "int32"), "nbu": ("sbuf", [128, 256], "uint16"),
    "f1": ("sbuf", [128, 128], "int32"), "f2": ("sbuf", [128, 128], "int32"), "f3": ("sbuf", [128, 128], "int32"),
    "rt": ("sbuf", [128, 256], "bfloat16"), "et": ("sbuf", [128, 256], "bfloat16"),
    "ro": ("sbuf", [128, 64], "float32"), "bL": ("sbuf", [128, 128], "bfloat16"), "dL": ("sbuf", [128, 64], "float32"),
    "DW": ("sbuf", [128, E], "bfloat16"),
    "C0": ("sbuf", [128, (NR - 1) * SQ], "bfloat16"), "L0": ("sbuf", [128, (NR - 1) * SQ], "bfloat16"),
    "W0": ("sbuf", [128, W], "bfloat16"), "Wx": ("sbuf", [128, 2 * W], "bfloat16"),
    "B0": ("sbuf", [128, NS], "bfloat16"), "Bx": ("sbuf", [128, NS], "bfloat16"),
    "GM": ("sbuf", [128, F * E], "bfloat16"), "G1": ("sbuf", [128, E], "float32"),
}
for _s in STREAMS:
    SCRATCH["snd" + _s] = ("sbuf", [128, 56], "uint16")
    for _n in ("nx", "nm", "of"):
        SCRATCH[_n + _s] = ("sbuf", [128, 128], "uint16")
    SCRATCH["tb" + _s] = ("sbuf", [128, TW], "bfloat16")
    SCRATCH["D0" + _s] = ("sbuf", [128, 2 * E], "bfloat16")
    SCRATCH["w1" + _s] = ("sbuf", [128, E], "bfloat16")
    SCRATCH["D1" + _s] = ("sbuf", [128, 2 * E], "float32")
    SCRATCH["Q" + _s] = ("sbuf", [128, 2 * E], "float32")
    SCRATCH["Y" + _s] = ("sbuf", [128, E], "float32")
for _x in LATER:
    SCRATCH["W" + _x] = ("sbuf", [128, W], "float32")
    SCRATCH["B" + _x] = ("sbuf", [128, NS // 2], "float32")
for _b in range(8):
    SCRATCH["pb%d" % _b] = ("psum", [128, 512], "float32")

SEMAPHORES = (["cv", "ca", "ct", "cg", "sent", "sentx", "mfar", "mnear"] + ["d%d" % k for k in range(30)]
              + ["ar%s_%d" % (x, t) for x in ["x"] + LATER for t in range(NR - 1)]
              + ["rl%s_%d" % (x, j) for x in ["x"] + LATER for j in range(4)])


def bits(engs):
    m = 0
    for e in engs:
        m |= 1 << e
    return m


def split(sets, n):
    while len(sets) < n:
        big = max(range(len(sets)), key=lambda q: (len(sets[q]), q))
        s0 = sets.pop(big)
        sets += [s0[:len(s0) // 2], s0[len(s0) // 2:]]
    return sets


def sides(T, topo, c):
    cores = list(T.cores)
    near = [d for d in cores if topo.chip(d) == topo.chip(c)]
    far = [d for d in cores if topo.chip(d) != topo.chip(c)]
    i = near.index(c)
    lo = topo.engines(c, far[0])
    hi = [e for e in topo.engines(c, near[(i + 1) % len(near)]) if e not in lo]
    return near, far, i, lo, hi


def small_plan(T, topo, c):
    near, far, i, lo, hi = sides(T, topo, c)
    fa = [far[(i + j) % len(far)] for j in range(len(far))]
    ne = [near[(i + j) % len(near)] for j in range(1, len(near))]
    return list(zip(fa, split([lo], len(fa)))), list(zip(ne, split([hi], len(ne))))


def make_plan(T, topo, plan, back=0):
    cores = list(T.cores)
    n = len(cores)
    calls, relay, arr, handed = {}, {}, {c: [] for c in cores}, []
    for r, c in enumerate(cores):
        near, far, i, lo, hi = sides(T, topo, c)
        over = [z for z in topo.cores_of(c) if topo.die(z) != topo.die(c) and z not in cores]
        beyond = [z for z in range(SIM) if z not in cores and topo.mates(topo.chip(z), topo.chip(far[0]))
                  and topo.may_write(z, far[0])]
        beyond.sort(key=lambda z: topo.die(z) != topo.die(c))
        owners = [a for a in near if topo.may_write(a, beyond[0])]
        mine = plan[sorted(near, key=lambda a: a in owners).index(c)].split()
        if back:
            over.reverse()
        used = {"far": 0, "n": 0}
        calls[c] = []
        for j, call in enumerate(mine):
            out = []
            for ways, engines in zip(call.split("|"), (lo, hi)):
                for way, engs in zip(ways, split([engines], max(1, len(ways)))):
                    if way == "n":
                        used["n"] += 1
                        d = near[(i + used["n"]) % len(near)]
                    else:
                        d = far[(i + used["far"]) % len(far)]
                        used["far"] += 1
                    t = (cores.index(d) - r) % n
                    ent = {"t": t, "to": d, "engs": engs, "tt": n - t - 1, "way": way, "key": (j, i), "next": None}
                    out.append(ent)
                    if way in "nA":
                        arr[d].append((j + (0.5 if way == "A" else 0), n - t - 1, len(engs)))
                    else:
                        across = [z for z in beyond if topo.die(z) != topo.die(c)]
                        stops = {"B": [over], "C": [beyond],
                                 "D": [[z for z in over if topo.may_write(z, across[0])], across]}[way]
                        handed.append((ent, stops))
            calls[c].append(out)
    for ent, stops in sorted(handed, key=lambda h: (-len(h[1]), h[0]["key"])):
        d = ent["to"]
        for hop, choice in enumerate(stops):
            z = min(choice, key=lambda z: len(relay.get(z, [])))
            nxt = {"to": d, "tt": ent["tt"], "key": (ent["key"][0] + hop * LATE, ent["key"][1]), "next": None,
                   "count": len(ent["engs"]) if hop == 0 else len(topo.engines(at, z))}
            relay.setdefault(z, []).append(nxt)
            ent["to"], ent["next"] = z, nxt
            ent, at = nxt, z
        arr[d].append((ent["key"][0] + LATE, ent["tt"], len(topo.engines(at, d))))
    for z in relay:
        relay[z].sort(key=lambda e: e["key"])
        for j, e in enumerate(relay[z]):
            e["slot"] = j
    for c in cores:
        arr[c].sort()
    return calls, relay, arr


def landing(T, x, e):
    n = S if x == "x" else SH
    if e["next"]:
        j = e["next"]["slot"]
        return T["B" + x][:, j * n:(j + 1) * n], "rl%s_%d" % (x, j)
    col = E + e["tt"] * S
    return T["W" + x][:, col:col + n], "ar%s_%d" % (x, e["tt"])


def helper_program(g, core, T, topo, plans):
    sent = 0
    for x in ["x"] + LATER:
        n = S if x == "x" else SH
        for e in plans[x][1].get(core, []):
            j = e["slot"]
            g.wait_ge(T.sem["rl%s_%d" % (x, j)], e["count"])
            rid, pid, _ = topo.addr(e["to"])
            dst, sem = landing(T, x, e)
            g.remote_dma(dst, T["B" + x][:, j * n:(j + 1) * n], T.sem[sem], T.sem.sent, pid, rid,
                         topo.mask(core, e["to"]))
            sent += len(topo.engines(core, e["to"]))
    if sent:
        g.wait_ge(T.sem.sent, sent)


def rank_program(g, core, T, topo):
    plans = {"x": make_plan(T, topo, PLAN_X)}
    by_stream = {s: make_plan(T, topo, PLAN_M, si) for si, s in enumerate(STREAMS)}
    for x in LATER:
        plans[x] = by_stream[x[1]]
    rank = T.rank_of(core)
    if rank is None:
        helper_program(g, core, T, topo, plans)
        return
    A, ACT = AluOpType, ActivationFunctionType
    Q = {"g": g, "v": g.vector, "a": g.scalar, "t": g.tensor, "s": g.sync}
    known = {q: {} for q in Q}
    total, snap, hist = {}, {}, {}
    ndma = [0]

    def order(q, reads, writes):
        need = {}
        for lst, wr in ((reads, False), (writes, True)):
            for key, lo, hi in lst:
                ps = key.startswith("pb")
                for (l2, h2, w2, q2, tok) in hist.get(key, []):
                    if ps:
                        hit = (q2 != q) or (q != "t" and (wr or w2) and l2 < hi and lo < h2)
                    else:
                        hit = (wr or w2) and l2 < hi and lo < h2
                    if hit:
                        need[tok[0]] = max(need.get(tok[0], 0), tok[1])
        for sem, val in sorted(need.items(), key=lambda kv: -len(snap.get(kv, {}))):
            if known[q].get(sem, 0) < val:
                Q[q].wait_ge(T.sem[sem], val)
                known[q][sem] = val
                for s2, v2 in snap.get((sem, val), {}).items():
                    if known[q].get(s2, 0) < v2:
                        known[q][s2] = v2

    def note(q, reads, writes, tok):
        snap[tok] = dict(known[q])
        for key, lo, hi in writes:
            keep = [h for h in hist.get(key, []) if not (lo <= h[0] and h[1] <= hi)]
            hist[key] = keep + [(lo, hi, True, q, tok)]
        for key, lo, hi in reads:
            hist.setdefault(key, []).append((lo, hi, False, q, tok))

    def op(q, fn, reads, writes):
        order(q, reads, writes)
        sem = "c" + q
        total[sem] = total.get(sem, 0) + 1
        fn().then_inc(T.sem[sem], 1)
        note(q, reads, writes, (sem, total[sem]))

    def dma(q, out, in_, reads, writes):
        order(q, reads, writes)
        sem = "d%d" % ndma[0]
        ndma[0] += 1
        total[sem] = 16
        Q[q].dma_start(out, in_).then_inc(T.sem[sem], 16)
        note(q + "d", reads, writes, (sem, 16))

    known["sd"], known["ad"] = known["s"], known["a"]
    vec, act, pe = g.vector, g.scalar, g.tensor
    pb = [T["pb%d" % b] for b in range(8)]
    IB, IBK = T.ZI[:, 16:144], ("ZI", 0, 160)
    half = (slice(0, HP), slice(HP, 2 * HP))
    NCH = range(len(CH))

    def mm(b, lo, hi, lhsT, rhs, start, stop, reads):
        op("t", lambda: pe.matmul(pb[b][:, lo:hi], lhsT, rhs, start, stop), reads, [("pb%d" % b, lo, hi)])

    def evict(q, name, a, b, lo, n, relu=False):
        out, src = T[name][:, a:a + n], pb[b][:, lo:lo + n]
        if q == "a":
            fn = lambda: act.activation(out, src, ACT.Relu if relu else ACT.Copy)
        elif relu:
            fn = lambda: vec.tensor_scalar(out, src, 0.0, None, A.max)
        else:
            fn = lambda: vec.tensor_copy(out, src)
        op(q, fn, [("pb%d" % b, lo, lo + n)], [(name, a, a + n)])

    def gather(q, out, okey, win, wkeys, offs, fkeys, scale=None):
        src = win.indirect(offs)
        if q == "a":
            if scale is None:
                fn = lambda: act.activation(out, src, ACT.Copy)
            else:
                fn = lambda: act.activation(out, src, ACT.Copy, scale=scale)
        elif scale is None:
            fn = lambda: vec.tensor_copy(out, src)
        else:
            fn = lambda: vec.tensor_scalar(out, src, scale, None, A.mult)
        op(q, fn, wkeys + fkeys, [okey])

    def piece(q, x, t):
        a = (t - 1) * S
        gather(q, T["B" + x][:, a:a + S], ("B" + x, a, a + S), T["W" + x][:, 0:E], [("W" + x, 0, E)],
               T.sndu[:, (t - 1) * 16:t * 16], [("sndu", 0, 112)])

    def send(trs, local):
        order("g", [x[4] for x in trs], [])
        out = []
        for to, engs, sem, src, _, dst in trs:
            rid, pid, _ = topo.addr(to)
            out.append(RemoteDMATransfer(dst_ids=[DstId(rid=rid, pnc=pid)], dma_engine_mask=bits(engs),
                                         remote_sem=T.sem[sem], src=src, dst=dst))
            total[local] = total.get(local, 0) + len(engs)
        g.remote_dma_fused(out, local_sem=T.sem[local])

    def pieces(x, who, lo=0, hi=NR):
        for k, e in enumerate([e for call in plans[x][0][core] for e in call][lo:hi]):
            piece(who[k % len(who)], x, e["t"])

    def calls(x, lo=0, hi=NR):
        B, n = T["B" + x], S if x == "x" else SH
        for call in plans[x][0][core][lo:hi]:
            trs = []
            for e in call:
                a = (e["t"] - 1 if x == "x" else turns.index(e["t"])) * n
                dst, sem = landing(T, x, e)
                trs.append((e["to"], e["engs"], sem, B[:, a:a + n], ("B" + x, a, a + n), dst))
            send(trs, "sentx" if x == "x" else "sent")

    turns = [e["t"] for call in plans[LATER[0]][0][core] for e in call]

    def exchange(x, who):
        lo = 0
        for q, n in who.split():
            hi = lo + int(n)
            gather(q, T["B" + x][:, lo * SH:hi * SH], ("B" + x, lo * SH, hi * SH), T["W" + x][:, 0:E], [("W" + x, 0, E)],
                   T["snd" + x[1]][:, lo * 8:hi * 8], [("snd%s%d" % (x[1], h), 0, 56) for h in range(2)])
            lo = hi
        calls(x)
        for _, tt, cnt in plans[x][2][core]:
            sem = "ar%s_%d" % (x, tt)
            total[sem] = cnt
            hist["W" + x].append((E + tt * S, E + tt * S + SH, True, "r", (sem, cnt)))

    dma("s", T.CI[32:64, 0:256], T.srcs[:], [], [("CI1", 0, 256)])
    dma("a", T.sndi[:], T.snd[:], [], [("sndi", 0, 112)])
    dma("s", T.CI[0:32, 0:256], T.dirs[:], [], [("CI0", 0, 256)])
    dma("s", T.Wx[:, 0:E], T.x[:], [], [("Wx", 0, E)])
    dma("s", T.CI[32:64, 256:512], T.dsts[:], [], [("CI1", 256, 512)])
    dma("s", T.CI[0:32, 256:512], T.dirs[:], [], [("CI0", 256, 512)])
    dma("s", T.nbi[:], T.nb[:], [], [("nbi", 0, 256)])

    def load_tab(si, after):
        for h in range(2):
            dma("s", T["tb" + STREAMS[si]][half[h], 0:D * D], T.tab[half[si], :], after,
                [("tb%s%d" % (STREAMS[si], h), 0, D * D)])
    load_tab(0, [])
    for h in range(2):
        dma("s", T.Wx[half[h], W:W + E], T.x[half[1 - h], :], [], [("Vx%d" % h, 0, E)])

    for name, n, val in (("ZI", 160, 1.0), ("RL", 512, 1.0), ("ZZ", 144, NODE)):
        op("v", lambda: vec.memset(T[name][:], val), [], [(name, 0, n)])
    for s in STREAMS:
        op("v", lambda: vec.memset(T["tb" + s][:, D * D:TW], 0.0), [], [("tz" + s, 0, 16)])
    for s in STREAMS:
        op("v", lambda: vec.memset(T["D0" + s][:, 0:2 * E:2], 0.0), [], [("Dz" + s, 0, E)])

    def sel(name, n, pattern, cmp, base, cm, fill=0.0):
        op("g", lambda: g.affine_select(T[name][:], T[name][:], pattern, cmp, fill, base, cm), [(name, 0, n)], [(name, 0, n)])
    sel("ZI", 160, [[-1, 160]], A.is_equal, 16, 1)
    sel("ZZ", 144, [[-16, 9], [1000, 16]], A.is_ge, -15000, 1)
    sel("RL", 512, [[-1, 4], [-4, 8], [-32, 16]], A.is_equal, 0, 1)
    sel("ZZ", 144, [[16, 9], [0, 16]], A.is_ge, 2, -1)
    sel("ZZ", 144, [[-16, 9], [1000, 16]], A.not_equal, -15000, 1, float(D))
    op("a", lambda: act.activation(T.IF[:], IB, ACT.Copy), [IBK], [("IF", 0, 128)])
    op("a", lambda: act.activation(T.I4[:], IB, ACT.Copy, scale=float(D * D)), [IBK], [("I4", 0, 128)])
    for h in range(2):
        for m in range(2):
            op("a", lambda: act.activation(T.DD[half[h], half[m]], T.ZI[half[h], 16 + h * HP:16 + (h + 1) * HP], ACT.Copy),
               [IBK], [("DD%d" % h, m * HP, (m + 1) * HP)])
    DDK = [("DD0", 0, 128), ("DD1", 0, 128)]
    op("a", lambda: act.activation(T.SF[:], T.DD[:], ACT.Copy), DDK, [("SF", 0, 128)])

    def rounded(lo):
        hi = lo + 256
        op("v", lambda: vec.tensor_copy(T.CB[0:64, lo:hi], T.CI[0:64, lo:hi]),
           [("CI0", lo, hi), ("CI1", lo, hi)], [("CB0", lo, hi)])

    def rest(lo):
        hi = lo + 256
        op("v", lambda: vec.tensor_tensor(T.CB[64:96, lo:hi], T.CI[32:64, lo:hi], T.CB[32:64, lo:hi], A.subtract),
           [("CI1", lo, hi), ("CB0", lo, hi)], [("CB1", lo, hi)])

    def rows(lo, b0):
        hi = lo + 256
        for q in range(4):
            mm(b0 + q // 2, (q % 2) * 256, (q % 2) * 256 + 256, T.RL[0:96, q * 128:(q + 1) * 128], T.CB[0:96, lo:hi],
               True, True, [("RL", 0, 512), ("CB0", lo, hi), ("CB1", lo, hi)])

    op("v", lambda: vec.tensor_copy(T.sndu[:], T.sndi[:]), [("sndi", 0, 112)], [("sndu", 0, 112)])
    pieces("x", "a", 0, X_EARLY)
    calls("x", 0, X_EARLY)
    rounded(0)
    op("v", lambda: vec.tensor_tensor(T.SB[:], T.DD[:], IB, A.subtract), DDK + [IBK], [("SB", 0, 128)])
    rest(0)
    rows(0, 0)
    rounded(256)
    evict("v", "W0", 0, 0, 0, H)
    evict("a", "W0", H, 1, 0, H)
    rest(256)
    rows(256, 6)

    cores = list(T.cores)
    mine = small_plan(T, topo, core)

    def small(part, sem, bank0, step):
        ts = [(cores.index(d) - rank) % NR for d, _ in part]
        c0 = 0 if sem == "mfar" else len(mine[0]) * SQ
        hf = (len(ts) + 1) // 2
        turn = sorted(range(len(ts)), key=lambda j: (j % hf, j))
        if step == "fold":
            for j in turn:
                piece("va"[j // hf], "0", ts[j])
            for j in turn:
                for q in range(4):
                    a = (ts[j] - 1) * S + q * SQ
                    mm(bank0 + j // hf, (j % hf) * SQ, (j % hf + 1) * SQ, T.ZI[:, 16 - 4 * q:144 - 4 * q],
                       T.B0[:, a:a + SQ], q == 0, q == 3, [IBK, ("B0", a, a + SQ)])
            return
        evict("v", "C0", c0, bank0, 0, hf * SQ)
        evict("a", "C0", c0 + hf * SQ, bank0 + 1, 0, (len(ts) - hf) * SQ)
        send([(d, engs, sem, T.C0[:, c0 + j * SQ:c0 + (j + 1) * SQ], ("C0", c0 + j * SQ, c0 + (j + 1) * SQ),
               T.L0[:, (NR - ts[j] - 1) * SQ:(NR - ts[j]) * SQ]) for j, (d, engs) in enumerate(part)], "sentx")
    small(mine[0], "mfar", 2, "fold")
    small(mine[1], "mnear", 4, "fold")
    pieces("x", "a", X_EARLY, X_EARLY + 1)
    small(mine[0], "mfar", 2, "send")
    pieces("x", "va", X_EARLY + 1, X_EARLY + 3)
    small(mine[1], "mnear", 4, "send")
    landed = {"mfar": [], "mnear": []}
    for q0 in cores:
        for part, sem in zip(small_plan(T, topo, q0), ("mfar", "mnear")):
            for d, engs in part:
                if d == core:
                    total[sem] = total.get(sem, 0) + len(engs)
                    landed[sem].append((cores.index(q0) - rank) % NR - 1)
    for sem in landed:
        for tt in landed[sem]:
            hist.setdefault("L0", []).append((tt * SQ, tt * SQ + SQ, True, "r", (sem, total[sem])))
    pieces("x", "va", X_EARLY + 3)
    calls("x", X_EARLY)
    for _, tt, cnt in plans["x"][2][core]:
        total["arx_%d" % tt] = cnt
        hist["Wx"].append((E + tt * S, E + tt * S + S, True, "r", ("arx_%d" % tt, cnt)))

    evict("a", "DW", 0, 6, 0, H)
    evict("v", "DW", H, 7, 0, H)
    op("v", lambda: vec.tensor_copy(T.nbu[:], T.nbi[:]), [("nbi", 0, 256)], [("nbu", 0, 256)])
    when = {tt: w for w, tt, _ in plans["x"][2][core]}
    late = [tt for _, tt, _ in plans["x"][2][core][-2:]]
    runs = []
    for tt in range(NR - 1):
        if tt in late:
            continue
        if runs and runs[-1][1] == tt:
            runs[-1][1] += 1
        else:
            runs.append([tt, tt + 1])
    for lo, hi in sorted(runs, key=lambda r: max(when[tt] for tt in range(*r))):
        a, b = E + lo * S, E + hi * S
        for h in range(2):
            dma("s", T.Wx[half[h], W + a:W + b], T.Wx[half[1 - h], a:b], [("Wx", a, b)], [("Vx%d" % h, a, b)])
    load_tab(1, [])
    for si, s in enumerate(STREAMS):
        for h in range(2):
            op("v", lambda: vec.tensor_scalar(T["nx" + s][half[h], :], T.nbi[half[si], h * 128:(h + 1) * 128],
                                              float(0 if h == si else W), None, A.add),
               [("nbi", 0, 256)], [("nx%s%d" % (s, h), 0, 128)])
    for h in range(16):
        mm(0, 0, 64, T.ZZ[:, 15 - h:143 - h], T.DW[:, h:E:16], h == 0, h == 15, [("ZZ", 0, 144), ("DW", 0, E)])
    op("v", lambda: vec.tensor_scalar(T.ro[:], pb[0][:, 0:64], ROUND64, ROUND64, A.add, A.subtract),
       [("pb0", 0, 64)], [("ro", 0, 64)])
    lo = 0
    for hi in range(1, NR):
        if hi == NR - 1 or turns[hi] != turns[hi - 1] + 1:
            op("v", lambda: vec.tensor_copy(T.sndp[:, lo:hi, :], T.sndi[:, turns[lo] - 1:turns[hi - 1], :]),
               [("sndi", 0, 112)], [("sndp", lo, hi)])
            lo = hi
    op("v", lambda: vec.tensor_tensor(T.dL[:], T.ro[:], pb[0][:, 0:64], A.subtract), [("pb0", 0, 64), ("ro", 0, 64)],
       [("dL", 0, 64)])
    for u in range(2):
        op("a", lambda: act.activation(T.bL[:, u * 64:u * 64 + 64], T.ro[:], ACT.Copy, scale=1.0 / D), [("ro", 0, 64)],
           [("bL", u * 64, u * 64 + 64)])

    nb0 = 0
    for sem in ("mfar", "mnear"):
        for j, tt in enumerate(landed[sem]):
            bank = 1 + nb0 + j
            for q in range(4):
                mm(bank, q * SQ, (q + 1) * SQ, T.ZI[:, 16 + 4 * q:144 + 4 * q], T.L0[:, tt * SQ:(tt + 1) * SQ], True, True,
                   [IBK, ("L0", tt * SQ, (tt + 1) * SQ)])
            evict("av"[j % 2], "W0", E + tt * S, bank, 0, S)
        nb0 += len(landed[sem])

    def meta(q, c, part=None):
        a, b = (c * E, c * E + GM_A[c]) if q == "a" else (c * E + GM_A[c], (c + 1) * E)
        if part is not None:
            a, b = ((a, (a + b) // 2), ((a + b) // 2, b))[part]
        gather(q, T.GM[:, a:b], ("GM", a, b), T.W0[:], [("W0", 0, W)], T.nbu[:, a // 16:b // 16], [("nbu", 0, 256)])

    def turn_meta(c):
        lo = (c // 2) * 64
        mm(4 + c % 2, lo, lo + 64, T.IF[:], T.dL[:], True, False, [("IF", 0, 128), ("dL", 0, 64)])
        for h in range(16):
            mm(4 + c % 2, lo, lo + 64, T.ZZ[:, 15 - h:143 - h], T.GM[:, c * E + h:(c + 1) * E:16],
               False, h == 15, [("ZZ", 0, 144), ("GM", c * E, (c + 1) * E)])

    def rounded_z(j):
        a, b = j * 128, j * 128 + 128
        op("v", lambda: vec.tensor_scalar(T.rt[:, a:b], pb[4 + j][:, 0:128], ROUND64, ROUND64, A.add, A.subtract),
           [("pb%d" % (4 + j), 0, 128)], [("rt", a, b)])

    def reverse(j):
        a, b = j * 128, j * 128 + 128
        op("v", lambda: vec.tensor_tensor(T.et[:, a:b], pb[4 + j][:, 0:128], T.rt[:, a:b], A.is_equal),
           [("pb%d" % (4 + j), 0, 128), ("rt", a, b)], [("et", a, b)])

    def offsets(j):
        a, b = j * 128, j * 128 + 128
        mm(6 + j, 0, 128, IB, T.bL[:], True, False, [IBK, ("bL", 0, 128)])
        mm(6 + j, 0, 128, IB, T.rt[:, a:b], False, False, [IBK, ("rt", a, b)])
        mm(6 + j, 0, 128, T.I4[:], T.et[:, a:b], False, True, [("I4", 0, 128), ("et", a, b)])

    def offset_lists(j, si):
        s = STREAMS[si]
        for h in range(2):
            op("v", lambda: vec.tensor_scalar(T["of" + s][half[h], j * 64:j * 64 + 64], pb[6 + j][half[si], h * 64:h * 64 + 64],
                                              float(D * D), None, A.min),
               [("pb%d" % (6 + j), h * 64, h * 64 + 64)], [("of%s%d" % (s, h), j * 64, j * 64 + 64)])

    def later_lists():
        v, vk = T.nbi[:, 128:256], ("nbi", 0, 256)
        op("v", lambda: vec.tensor_scalar(T.f1[:], v, SH, None, A.bitwise_and), [vk], [("f1", 0, 128)])
        op("v", lambda: vec.tensor_scalar(T.f2[:], v, float(E), None, A.is_ge), [vk], [("f2", 0, 128)])
        op("v", lambda: vec.tensor_scalar(T.f1[:], T.f1[:], -2.0, float(SH), A.mult, A.add), [("f1", 0, 128)], [("f1", 0, 128)])
        for si, s in enumerate(STREAMS):
            op("v", lambda: vec.tensor_copy(T["nm" + s][half[0], :], T.nbi[half[si], 0:128]), [vk], [("nm%s0" % s, 0, 128)])
        op("v", lambda: vec.tensor_tensor(T.f3[:], T.f1[:], T.f2[:], A.mult), [("f1", 0, 128), ("f2", 0, 128)], [("f3", 0, 128)])
        op("v", lambda: vec.tensor_tensor(T.f2[:], T.f3[:], v, A.add), [("f3", 0, 128), vk], [("f2", 0, 128)])
        for si, s in enumerate(STREAMS):
            op("v", lambda: vec.tensor_copy(T["nm" + s][half[1], :], T.f2[half[si], :]), [("f2", 0, 128)], [("nm%s1" % s, 0, 128)])

    def edges(i):
        return CH[i] if isinstance(i, int) else (CH[i[0]][0], CH[i[-1]][1])

    def listed(name, s, j, i):
        a, b = edges(i)
        lo, hi = j * 64 + a // 16, j * 64 + b // 16
        return T[name + s][:, lo:hi], [("%s%s%d" % (name, s, h), lo, hi) for h in range(2)]

    def wplace(s, j, i):
        a, b = edges(i)
        if j == 0:
            return T["D0" + s][:, 2 * a + 1:2 * b:2], ("Dw" + s, a, b)
        return T["w1" + s][:, a:b], ("w1" + s, a, b)

    def term(s, j, i):
        a, b = edges(i)
        return T["D1" + s][:, 2 * a + j:2 * b:2], ("D1%s%d" % (s, j), a, b)

    def window(k, s):
        if k == 1:
            return T.Wx[:], [("Wx", 0, 2 * W), ("Vx0", 0, W), ("Vx1", 0, W)], "nx"
        return T["W%d%s" % (k, s)][:], [("W%d%s" % (k, s), 0, W)], "nm"

    def weight(q, s, j, i):
        offs, fk = listed("of", s, j, i)
        out, ok = wplace(s, j, i)
        gather(q, out, ok, T["tb" + s][:], [("tb%s0" % s, 0, TW), ("tb%s1" % s, 0, TW), ("tz" + s, 0, 16)], offs, fk, 0.25)

    def fetch(q, k, s, j, i):
        win, wk, ln = window(k, s)
        offs, fk = listed(ln, s, j, i)
        a, b = CH[i]
        out, ok = term(s, 0, i) if j == 0 else (T.G1[:, a:b], ("G1", a, b))
        gather(q, out, ok, win, wk, offs, fk)

    def hold(s):
        a, b = CH[HELD]
        mm(6 + STREAMS.index(s), 0, b - a, IB, T["w1" + s][:, a:b], True, True, [IBK, ("w1" + s, a, b)])

    def times(s, i):
        a, b = CH[i]
        bank, lo = 6 + STREAMS.index(s), 0
        out, ok = term(s, 1, i)
        op("v", lambda: vec.tensor_tensor(out, pb[bank][:, lo:lo + b - a], T.G1[:, a:b], A.mult),
           [("pb%d" % bank, lo, lo + b - a), ("G1", a, b)], [ok])

    def fused(k, s, j, i):
        win, wk, ln = window(k, s)
        offs, fk = listed(ln, s, j, i)
        out, ok = term(s, j, i)
        wv, wkey = wplace(s, j, i)
        op("v", lambda: vec.tensor_tensor(out, win.indirect(offs), wv, A.mult), wk + fk + [wkey], [ok])

    def scan(s, i):
        a, b = CH[i]
        op("v", lambda: vec.tensor_tensor_scan(T["Q" + s][:, 2 * a:2 * b], T["D0" + s][:, 2 * a:2 * b],
                                               T["D1" + s][:, 2 * a:2 * b], 0.0, A.mult, A.add),
           [("Dz" + s, a, b), ("Dw" + s, a, b), ("D1%s0" % s, a, b), ("D1%s1" % s, a, b)], [("Q" + s, a, b)])

    def pe_x(s, i, b0):
        a, b = CH[i]
        si = STREAMS.index(s)
        mm(b0 + i, 0, b - a, T.DD[half[si], :], T.Wx[half[si], a:b], True, False, [("DD%d" % si, 0, 128), ("Wx", a, b)])

    def pe_term(s, j, i, b0, stop):
        a, b = CH[i]
        src, key = term(s, j, i)
        mm(b0 + i, 0, b - a, T.SF[:], src, False, stop, [("SF", 0, 128), key])

    def pe_q(s, i, b0):
        a, b = CH[i]
        mm(b0 + i, 0, b - a, T.SF[:], T["Q" + s][:, 2 * a + 1:2 * b:2], False, True, [("SF", 0, 128), ("Q" + s, a, b)])

    def done(q, k, s, i, b0):
        a, b = CH[i]
        evict(q, "W%d%s" % (k + 1, s) if k < 4 else "Y" + s, a, b0 + i, 0, b - a, relu=True)

    waiting = {x: list(plans[x][2][core]) for x in LATER}

    def copies(who, x, n):
        for ent in waiting[x][:n]:
            waiting[x].remove(ent)
            col = E + ent[1] * S
            for h in range(2):
                q = who[h % len(who)]
                out, src = T["W" + x][half[h], col + SH:col + S], T["W" + x][half[1 - h], col:col + SH]
                op(q, (lambda: vec.tensor_copy(out, src)) if q == "v" else (lambda: act.activation(out, src, ACT.Copy)),
                   [("W" + x, col, col + SH)], [("W" + x, col + SH + h * HP, col + SH + (h + 1) * HP)])

    def x_across(j, q):
        col = E + late[j] * S
        mm(3 - j, 0, S, T.SB[:], T.Wx[:, col:col + S], True, True, [("SB", 0, 128), ("Wx", col, col + S)])
        evict(q, "Wx", W + col, 3 - j, 0, S)

    for c in (1, 3, 0):
        meta("a", c)
        meta("v", c)
        turn_meta(c)
    meta("a", 2)
    meta("v", 2, 0)
    rounded_z(1)
    meta("v", 2, 1)
    reverse(1)
    offsets(1)
    turn_meta(2)
    for si, s in enumerate(STREAMS):
        for h in range(2):
            op("v", lambda: vec.tensor_copy(T["snd" + s][half[h], :], T.sndp[half[si], :, h * 8:(h + 1) * 8]),
               [("sndp", 0, NR - 1)], [("snd%s%d" % (s, h), 0, 56)])
    offset_lists(1, 0)
    weight("a", "a", 1, NCH[2:])
    rounded_z(0)
    x_across(0, "v")
    reverse(0)
    x_across(1, "a")
    offsets(0)

    def sums(s, j, span):
        for i in span:
            if j == 1:
                pe_x(s, i, 4 * STREAMS.index(s))
            pe_term(s, j, i, 4 * STREAMS.index(s), j == 0)

    def first(s, j, span, weights=True, summed=True):
        if weights:
            weight("a", s, j, span)
        fused(1, s, j, span)
        if summed:
            sums(s, j, span)

    first("a", 1, NCH[2:], False)
    offset_lists(0, 0)
    first("a", 1, [1])
    first("a", 1, [0])
    offset_lists(1, 1)
    for i in NCH:
        first("a", 0, [i])
    offset_lists(0, 1)
    first("b", 1, [0])
    first("b", 1, [1])
    first("b", 1, NCH[2:], True, False)
    for i in NCH:
        done("a", 1, "a", i, 0)
    exchange("2a", WHO_A)
    sums("b", 1, NCH[2:])
    for span in ([0], [1], NCH[2:]):
        first("b", 0, span)
    later_lists()
    for i in NCH:
        done("a", 1, "b", i, 4)
    for s in STREAMS:
        hold(s)
    copies("v", "2a", NR)
    exchange("2b", WHO_M)

    for x, nxt in zip(LATER, LATER[1:] + [None]):
        k, s = int(x[0]), x[1]
        si = STREAMS.index(s)

        def finish(i):
            done("a", k, s, i, 0)
            if k == 4 and i in (1, 3):
                a, b = CH[i - 1][0], CH[i][1]
                dma("s", T.y[half[si], a:b], T["Y" + s][half[0], a:b], [("Y" + s, a, b)], [])
            if x == LATER[-2]:
                copies("a", nxt, EARLY[i])
        for i in NCH:
            pe_x(s, i, 0)

        def scanned(i):
            scan(s, i)
            pe_q(s, i, 0)
            finish(i)
        fetch("a", k, s, 1, HELD)
        for i in NCH[1:]:
            fetch("a", k, s, 0, i)
        fused(k, s, 1, 0)
        pe_term(s, 1, 0, 0, False)
        fused(k, s, 1, 1)
        fused(k, s, 0, 0)
        pe_term(s, 0, 0, 0, True)
        finish(0)
        times(s, HELD)
        scanned(1)
        fused(k, s, 1, 3)
        scanned(2)
        scanned(3)
        if nxt:
            copies("v", nxt, NR if nxt != LATER[-1] else LAST_V)
        if nxt == LATER[-1]:
            copies("va", nxt, NR)
        if k < 4:
            exchange(str(k + 1) + s, WHO_M)

    for sem in sorted(total):
        g.wait_ge(T.sem[sem], total[sem])
